import numpy as np, ml_dtypes
CORES = [40,64,80,88,96,104,120,144]
N = 8
import mx_ref
BF = ml_dtypes.bfloat16
def gcols(t, e):
    v = np.concatenate([t.reshape(8, 16, -1, 4), np.zeros((8, 16, 1, 4), BF)], axis=2)
    return np.ascontiguousarray(np.stack([v[g][:, e[g]] for g in range(8)])).reshape(128, -1)
def tile(rs):
    return np.stack(rs, axis=2).reshape(128, -1).astype(BF)
def pick(q, e):
    c = np.concatenate([q[0].reshape(128, -1, 4), np.zeros((128, 1, 4), np.uint8)], axis=1); s = np.concatenate([q[1], np.ones((16, 1), np.uint8)], axis=1)
    return (np.ascontiguousarray(c[:, e].reshape(128, -1)), np.ascontiguousarray(s[:, e]))
def join(*qs):
    return (np.concatenate([q[0] for q in qs], axis=1), np.concatenate([q[1] for q in qs], axis=1))
def put(q, e, v):
    c, s = q[0].reshape(128, -1, 4).copy(), q[1].copy(); c[:, e] = v[0].reshape(128, -1, 4); s[:, e] = v[1]
    return (c.reshape(128, -1), s)
def pk(c, s):
    return (np.ascontiguousarray(c), mx_ref.live(s))
def emit(q):
    return q[0], q[1]
def packed(v, rng):
    q = [mx_ref.quantize(np.ascontiguousarray(v[r])) for r in range(N)]
    return np.stack([a for a, b in q]), np.stack([mx_ref.plane(b, rng) for a, b in q])
def values_of_codes():
    e, c = np.zeros((128, 128, 4), np.float32), np.zeros((128, 2, 4), np.uint8)
    e[np.arange(128), np.arange(128), 0] = 1
    c[:127, :, 0] = np.arange(256).reshape(2, 128).T[:127]
    return mx_ref.matmul(mx_ref.quantize(e.reshape(128, 512).astype(BF)), (c.reshape(128, 8), np.full((16, 2), 127, np.uint8))).T.reshape(-1).astype(np.float64)
CODE_VALUE, SCALE_VALUE = values_of_codes(), 2.0 ** (np.arange(256) - 127.0)
def decode(q):
    return (CODE_VALUE[q[0]].reshape(16, 8, -1, 4) * SCALE_VALUE[q[1]][:, None, :, None] + 0.0).reshape(128, -1).astype(np.float32)
def f(rng, *shape):
    return mx_ref.flush((rng.standard_normal(shape, dtype=np.float32) * np.exp2(rng.integers(-2, 3, shape[:-1] + (1,)))).astype(BF))
def wide(rng, *shape, cols=0):
    v = rng.standard_normal(shape, dtype=np.float32) * np.exp2(rng.integers(-12, 13, shape)).astype(np.float32)
    if cols: v *= np.repeat(np.exp2(rng.integers(-cols, cols + 1, shape[:-2] + (1, shape[-1] // 4))) * (rng.random(shape[:-2] + (1, shape[-1] // 4)) > 0.0625), 4, axis=-1).astype(np.float32)
    return mx_ref.flush(v.astype(BF))
C, R = 256, 3
STEP = [1, 2, 4]
DOUBLINGS = 8
def order(p):
    return np.argsort(-(p + np.float32(0.0)), axis=1, kind="stable")
def mates(o):
    m = np.zeros_like(o)
    np.put_along_axis(m, o, np.ascontiguousarray(o.reshape(8, -1, 2)[:, :, ::-1]).reshape(8, -1), axis=1)
    return m
def at(a, e):
    return np.take_along_axis(a, e, axis=1)
def big(v):
    v = v.astype(np.float32)
    v[np.abs(v) < np.float32(2.0 ** -16)] = 0
    return v.astype(BF)
def same(u):
    return np.stack([u.reshape(128, 512)] * N)
def numbers_of(rng):
    return {"x": big(f(rng, N, 128, 4 * C)), "u": same(np.array(f(rng, 128, 512))), "v": np.array(f(rng, N, 128, 512))}
def weights(rng, w):
    c, p = packed(w, rng)
    return {"wc": c, "ws": p}
def still(rng):
    return weights(rng, np.zeros((N, 128, 2048), BF))
def ring(rng):
    v = np.concatenate([rng.permutation(C), C + rng.permutation(C)]).reshape(C, 2)[rng.permutation(C)].reshape(-1)
    a, b = np.zeros(2 * C, int), np.zeros(2 * C, int)
    a[v[v < C]] = np.arange(C)
    a[v[v >= C]] = np.arange(C)
    b[np.roll(v, -1).reshape(C, 2)[rng.permutation(C)].reshape(-1)] = np.arange(2 * C)
    return a, b
def digits(s):
    return (((s[:, None] >> np.arange(12)) & 1) * 2.0 ** (np.arange(12) - 23.0)).reshape(-1, 3, 4).transpose(1, 0, 2)
def setup_inputs(rng):
    return {**numbers_of(rng), **weights(rng, big(f(rng, N, 128, 2048)))}
def setup_inputs_ties(rng):
    d = numbers_of(rng)
    e = rng.permutation(N)
    x = d["x"].reshape(N, 8, 16, C, 4)
    a = x[0][:, :8, :3].copy()
    a[:, :, 2] = 0
    for r in range(N):
        k = np.zeros(C, int) if r == e[0] else rng.permutation(C) % 3
        x[r][:, :8] = a[:, :, k]
    x[e[1]] = 0
    u = d["u"][0].reshape(8, 16, 128, 4).copy()
    u[:, 8:, ::8] = 0
    g = 16 * rng.permutation(8)
    u[:, :, g[:2]] = 0
    u[:, :, g[2:4] + 8] = 0
    u[:, :, [g[4], g[4] + 8]] = 0
    return {"x": x.reshape(N, 128, 4 * C), "u": same(u), "v": d["v"], **weights(rng, big(f(rng, N, 128, 2048)))}
def setup_inputs_near(rng):
    d = numbers_of(rng)
    x = d["x"].astype(np.float32).reshape(N, 8, 16, C, 4)
    o = rng.permutation(8)
    c = np.array([1.0, -1.0, 1.0, -1.0, 1.0, -1.0, 0.0, 0.0])[o]
    k = np.array([1.0, 1.0, 1.0, 1.0, 2.0 ** -30, 2.0 ** -30, 2.0 ** -30, -2.0 ** -30])[o].astype(np.float32).astype(BF)
    x[:, :, 0] = 0
    x[:, :, 0, :, 0] = c[None, :, None]
    x[:, :, 14:] = rng.integers(4, 8, (N, 8, 2, C, 4)) * rng.choice([-1.0, 1.0], (N, 8, 2, C, 4)) * 2.0 ** -20
    for i in range(0, N, 2):
        for g in range(8):
            a, b = ring(rng)
            for s in range(2):
                x[i + s, g, 8:11] = digits(a[C * s:C * s + C])
                x[i + s, g, 11:14] = digits(b[C * s:C * s + C])
    u = d["u"][0].reshape(128, 128, 4).copy()
    u[:, ::8] = 0
    for g in range(8):
        h = 16 * g
        u[h, h, 0] = k[g]
        u[h, h + 8, 0] = k[g]
        u[h + 8:h + 11, h] = k[g]
        u[h + 11:h + 14, h + 8] = k[g]
    return {"x": x.reshape(N, 128, 4 * C).astype(BF), "u": same(u), "v": d["v"], **still(rng)}
def setup_inputs_huge(rng):
    d = numbers_of(rng)
    c = np.ones((N, C))
    for i, k in enumerate(rng.permutation(N // 2) % 3):
        if k == 1: c[2 * i + int(rng.integers(2))] = -1
        if k == 2:
            for s in range(2): c[2 * i + s] = rng.permutation(C) % 2 * 2.0 - 1.0
    x = 2.0 ** 30 * (0.6 + 0.4 * rng.random((N, 128, C, 4))) * c[:, None, :, None]
    g = np.stack([rng.permutation(8) % 2, rng.permutation(8) % 2], axis=1).reshape(16) * 2.0 - 1.0
    u = d["u"][0].reshape(128, 128, 4).copy()
    u[:, ::8] = (2.0 ** 30 * (1 - 0.25 * rng.random((128, 16, 4))) * g[None, :, None]).astype(np.float32).astype(BF)
    return {"x": x.astype(np.float32).reshape(N, 128, 4 * C).astype(BF), "u": same(u), "v": d["v"], **still(rng)}
def setup_inputs_spread(rng):
    d = setup_inputs(rng)
    d["x"] = big(wide(rng, N, 128, 4 * C, cols=6))
    return d
def check_inputs(d):
    b = []
    for k in ("x", "u", "v"):
        a = np.abs(d[k].astype(np.float32))
        if not (np.isfinite(a).all() and ((a == 0) | (a >= 2.0 ** -30) & (a <= 2.0 ** 30)).all()): b.append("a value of " + k)
    if (d["u"] != d["u"][:1]).any(): b.append("u differs between ranks")
    if ((d["wc"] & 127) == 127).any(): b.append("a code of wc is no number")
    a = np.zeros((128, 4, 4), np.float32)
    a[:, 1] = 2.0 ** -30
    a[:, 2] = 2.0 ** 30
    e = emit(mx_ref.quantize(a.reshape(128, 16).astype(BF)))[1][0]
    s = np.stack([mx_ref.live(p) for p in d["ws"]])
    if not ((s == e[0]) | (s >= e[1]) & (s <= e[2])).all(): b.append("a scale of ws")
    return b
def reference(x, u, v, wc, ws):
    qu = mx_ref.quantize(u[0])
    lay = [pk(wc[r], ws[r]) for r in range(N)]
    now = [x[r] for r in range(N)]
    for t in range(R):
        num, s, sent, reds = [], [], [], [None] * N
        for r in range(N):
            q = mx_ref.quantize(now[r])
            num.append(decode(q).astype(BF))
            s.append(mx_ref.matmul(qu, q))
        own = [mates(order(s[r][::16])) for r in range(N)]
        for lo in range(N):
            hi = lo ^ STEP[t]
            if lo < hi:
                a = np.concatenate([own[lo], C + own[hi]], axis=1)
                b = mates(order(np.concatenate([s[lo][8::16], s[hi][8::16]], axis=1)))
                to = at(b, a)
                low = np.tile(np.arange(2 * C), (8, 1))
                for i in range(DOUBLINGS):
                    low = np.minimum(low, at(low, to))
                    to = at(to, to)
                blue = low > at(low, a)
                reds[lo] = np.argsort(blue[:, :C], axis=1, kind="stable")[:, :C // 2]
                reds[hi] = np.argsort(blue[:, C:], axis=1, kind="stable")[:, :C // 2]
        for r in range(N):
            one = gcols(num[r], reds[r]).astype(np.float32)
            two = gcols(num[r], at(own[r], reds[r])).astype(np.float32)
            sent.append(mx_ref.quantize(((one + two) * np.float32(0.5)).astype(BF)))
        for r in range(N):
            e = np.tile(np.arange(C), (8, 1))
            np.put_along_axis(e, reds[r], np.tile(C + np.arange(C // 2), (8, 1)), axis=1)
            came = decode(sent[r ^ STEP[t]]).astype(BF)
            z = mx_ref.quantize(gcols(np.concatenate([num[r], came], axis=1), e))
            d = decode(z).reshape(128, C, 4)
            now[r] = tile([d[:, :, b] + np.maximum(mx_ref.matmul(pick(lay[r], np.arange(128 * b, 128 * b + 128)), z), np.float32(0.0)) * np.float32(0.03125) for b in range(4)])
    y, ol = np.zeros((N, 128, C), np.float32), np.zeros((N, 8, C // 2), np.float32)
    oc, osc = np.zeros((N, 128, 4 * C), np.uint8), np.zeros((N, 16, C), np.uint8)
    for r in range(N):
        q = mx_ref.quantize(now[r])
        y[r] = mx_ref.matmul(mx_ref.quantize(v[r]), q)
        ol[r] = reds[r]
        oc[r], osc[r] = emit(q)
    return {"y": y, "ol": ol, "oc": oc, "osc": osc}

@@ -1,0 +1,541 @@
+from concourse.bass import DstId, RemoteDMATransfer
+from concourse.mybir import dt, AluOpType, ActivationFunctionType
+
+ALU = AluOpType
+ACT = ActivationFunctionType
+C = 256
+ROUNDS = 3
+STEP = [1, 2, 4]
+DOUBLINGS = 8
+OWN_S = 16
+CROSS_S = 4
+HALVES = 2
+BIG = 2.0 ** 40
+Q4, U8, BF, F32, I32, U16 = "float8_e4m3fn_x4", "uint8", "bfloat16", "float32", "int32", "uint16"
+
+SCRATCH = {}
+for _d, _l in [
+    (BF, "x0 1024 xn 1024 ub 512 vb 512 ones 512 eb 2048 t16 512 maskd 512 ceq 512 c0 512 cx 512 ctmp 16 iotaj 512 iotak 512 "
+         "nodet 512 wn 768 eqf 512 eqs 512 fa 4096 fb 4096 fo 4096 sa 2048 so 2048 sx 2048 sg 4096 sgx 4096 inva 512 invs 512 "
+         "arep 512 xs 512 xs2 512 xs3 512 mm 512 ms 512 pa 512 pb 512 lowa 512 lowb 512 lowc 512 fl 544 vv 512 nodep 256 yv 256 "
+         "dp 1536 dpp 1024 g1 512 bt 512 yt 1024"),
+    (Q4, "uq 128 upq 256 vq 128 wq 512 eq4 512 bq 128 zq 256 tq0 512 tq1 512 tq2 512 tq3 256"),
+    (U8, "us 128 ups 256 vs 128 wsc 512 es 512 bs 128 zs 256 ts0 512 ts1 512 ts2 512 ts3 256"),
+    (I32, "pcol 8 rcol 8 offi 16 cw0 16 cw 16 wi 32 hh 32 nf 32 tc 32 lm 32"),
+    (F32, "rf 8 rf1 8 scl 8 klo 16 khi 16 wo 768 sm 512 sc 512 accl 16 accg 16 accx 16 ke 16 dd 16 own 16 rbm 16 rr 1024 yo 256"),
+    (U16, "offu 16 evl 16 awl 32 ll 256 lu 32 yl 16 ol16 16 msg0 32 msg1 32 msg2 32 lb0 32 lb1 32 lb2 32"),
+]:
+    _w = _l.split()
+    for _i in range(0, len(_w), 2):
+        SCRATCH[_w[_i]] = ("sbuf", [128, int(_w[_i + 1])], _d)
+for _b in range(8):
+    SCRATCH["p%d" % _b] = ("psum", [128, 512], F32)
+
+SEMAPHORES = ["s_vector", "s_scalar", "s_tensor", "s_pool", "left"] + ["dma%d" % _k for _k in range(16)]
+for _t in range(ROUNDS):
+    SEMAPHORES += ["at%d" % _t, "as%d" % _t, "am%d" % _t, "ar%d" % _t, "aq%d" % _t]
+
+
+def _mask(engines):
+    m = 0
+    for e in engines:
+        m |= 1 << e
+    return m
+
+
+def relays(T, topo, src, dst):
+    r = [c for c in topo.cores_of(src) if c != src and T.rank_of(c) is None and topo.may_write(c, dst)]
+    r.sort(key=lambda c: (topo.die(c) != topo.die(src), c))
+    return r[:4]
+
+
+def pieces(t, hi):
+    o = 16 * hi
+    out = [(1 + k, "tq%d" % t, (128 * k, 128 * k + 128), (C + 128 * k, C + 128 * k + 128), "at%d" % t, True) for k in range(2)]
+    out.append((3, "ts%d" % t, (0, C), (C, 2 * C), "as%d" % t, False))
+    out.append((0, "msg%d" % t, (o, o + 16), (o, o + 16), "am%d" % t, False))
+    out.append((1, "lb%d" % t, (o + 8, o + 16), (o + 8, o + 16), "aq%d" % t, False))
+    out.append((0, "lb%d" % t, (o, o + 8), (o, o + 8), "ar%d" % t, False))
+    return out
+
+
+def view(T, name, cols, codes):
+    ap = T[name][:, cols[0]:cols[1]]
+    return ap.bitcast(dt.uint8) if codes else ap
+
+
+def relay_program(g, core, T, topo):
+    left = 0
+    for src in [c for c in topo.cores_of(core) if T.rank_of(c) is not None]:
+        r = T.rank_of(src)
+        for t in range(ROUNDS):
+            dst = T.cores[r ^ STEP[t]]
+            rel = relays(T, topo, src, dst)
+            for k, name, a, b, sem, codes in pieces(t, 1 if r & STEP[t] else 0):
+                if rel[k] != core:
+                    continue
+                n = len(topo.engines(src, core))
+                g.wait_ge(T.sem[sem], n // 2 if codes else n)
+                rid, pid = topo.addr(dst, core)
+                g.remote_dma(view(T, name, b, codes), view(T, name, b, codes), T.sem[sem], T.sem.left, pid, rid, topo.mask(core, dst))
+                left += len(topo.engines(core, dst))
+    if left:
+        g.wait_ge(T.sem.left, left)
+
+
+def clash(a, b):
+    if a[2] <= b[1] or b[2] <= a[1]:
+        return False
+    return not (a[3] > 1 and a[3] == b[3] and a[1] % a[3] != b[1] % b[3])
+
+
+def emit(g, T, ops, left):
+    queues = {"vector": g.vector, "scalar": g.scalar, "tensor": g.tensor, "pool": g, "sync": g.sync}
+    seen = {}
+    lines = {q: [] for q in queues}
+    for i, o in enumerate(ops):
+        deps = set()
+        regs = [(r, False) for r in o["r"]] + [(r, True) for r in o["w"]]
+        for reg, wr in regs:
+            bank = SCRATCH[reg[0]][0] == "psum"
+            for j, reg2, wr2 in seen.get(reg[0], []):
+                if (wr or wr2 or ops[j]["q"] != o["q"]) if bank else ((wr or wr2) and clash(reg, reg2)):
+                    deps.add(j)
+        for reg, wr in regs:
+            seen.setdefault(reg[0], []).append((i, reg, wr))
+        o["deps"] = deps
+        if o["kind"] == "c":
+            o["pos"] = len(lines[o["q"]])
+            lines[o["q"]].append(i)
+    waited = {q: {} for q in queues}
+    for o in ops:
+        o["waits"] = []
+        if o["kind"] == "arrive":
+            continue
+        want = {}
+        for j in o["deps"]:
+            p = ops[j]
+            if p["kind"] == "c":
+                want[p["q"]] = max(want.get(p["q"], -1), p["pos"])
+            elif p["kind"] in ("dma", "arrive"):
+                want[("x", j)] = 0
+        for key in sorted(want, key=str):
+            pos = want[key]
+            if waited[o["q"]].get(key, -1) >= pos:
+                continue
+            if key == o["q"] and o["kind"] == "c":
+                pos = max(pos, o["pos"] - 2)
+            waited[o["q"]][key] = pos
+            j = key[1] if isinstance(key, tuple) else lines[key][pos]
+            ops[j]["inc"] = True
+            o["waits"].append(j)
+    count = {q: 0 for q in queues}
+    ndma = 0
+    for o in ops:
+        if o["kind"] == "c" and o.get("inc"):
+            count[o["q"]] += 1
+            o["sem"], o["val"] = "s_" + o["q"], count[o["q"]]
+        elif o["kind"] == "dma":
+            o["sem"], o["val"] = "dma%d" % ndma, 16
+            ndma += 1
+    for o in ops:
+        if o["kind"] == "arrive":
+            continue
+        q = queues[o["q"]]
+        for j in o["waits"]:
+            q.wait_ge(T.sem[ops[j]["sem"]], ops[j]["val"])
+        ins = o["f"](q)
+        if o["kind"] == "dma":
+            ins.then_inc(T.sem[o["sem"]], 16)
+        elif o["kind"] == "c" and o.get("inc"):
+            ins.then_inc(T.sem[o["sem"]], 1)
+    for o in ops:
+        if o["kind"] == "dma" and not o.get("inc"):
+            queues[o["q"]].wait_ge(T.sem[o["sem"]], 16)
+    g.wait_ge(T.sem.left, left)
+
+
+def rank_program(g, core, T, topo):
+    rank = T.rank_of(core)
+    if rank is None:
+        relay_program(g, core, T, topo)
+        return
+    ops = []
+    left = [0]
+
+    def A(name, a=0, b=None, step=1):
+        if b is None:
+            b = SCRATCH[name][1][1]
+        return (T[name][:, a:b:step] if step > 1 else T[name][:, a:b], [(name, a, b, step)])
+
+    def G(win, off):
+        return (win[0].indirect(off[0]), win[1] + off[1])
+
+    def add(q, f, r, w, kind="c"):
+        ops.append({"q": q, "f": f, "r": [x for a in r if isinstance(a, tuple) for x in a[1]], "w": [x for a in w for x in a[1]], "kind": kind})
+
+    def ap(a):
+        return a[0] if isinstance(a, tuple) else a
+
+    def copy(out, in_):
+        add("vector", lambda q: q.tensor_copy(out[0], in_[0]), [in_], [out])
+
+    def scatter(win, off, in_):
+        add("vector", lambda q: q.tensor_copy(win[0].indirect(off[0]), in_[0]), [in_, off], [win])
+
+    def tt(out, a, b, op):
+        add("vector", lambda q: q.tensor_tensor(out[0], a[0], b[0], op), [a, b], [out])
+
+    def ts(out, a, s1, op0, s2=None, op1=None):
+        if op1 is None:
+            add("vector", lambda q: q.tensor_scalar(out[0], a[0], ap(s1), None, op0), [a, s1], [out])
+        else:
+            add("vector", lambda q: q.tensor_scalar(out[0], a[0], ap(s1), ap(s2), op0, op1), [a, s1, s2], [out])
+
+    def scan(out, d0, d1, init, op0, op1):
+        add("vector", lambda q: q.tensor_tensor_scan(out[0], d0[0], d1[0], ap(init), op0, op1), [d0, d1, init], [out])
+
+    def memset(out, v):
+        add("vector", lambda q: q.memset(out[0], v), [], [out])
+
+    def quant(cq, cs, in_):
+        add("vector", lambda q: q.quantize_mx(cq[0], cs[0], in_[0]), [in_], [cq, cs])
+
+    def act(out, in_, func, bias=None, scale=None, accum=None):
+        kw = {}
+        if bias is not None:
+            kw["bias"] = ap(bias)
+        if scale is not None:
+            kw["scale"] = scale
+        if accum is not None:
+            kw["accum_out"] = accum[0]
+        add("scalar", lambda q: q.activation(out[0], in_[0], func, **kw), [in_, bias], [out] + ([accum] if accum else []))
+
+    def mm(bank, lq, ls, la, rq, rs, ra, n):
+        out = A("p%d" % bank, 0, n)
+        a, b, c, d = A(lq, la, la + 128), A(ls, la, la + 128), A(rq, ra, ra + n), A(rs, ra, ra + n)
+        add("tensor", lambda q: q.matmul_mx(out[0], a[0], b[0], c[0], d[0], True, True), [a, b, c, d], [out])
+
+    def iota(out, pattern, base, cm, small=True):
+        if small:
+            add("pool", lambda q: q.iota(out[0], pattern, base, cm, allow_small_or_imprecise_dtypes=True), [], [out])
+        else:
+            add("pool", lambda q: q.iota(out[0], pattern, base, cm), [], [out])
+
+    def unit(b):
+        out = A("eb", 512 * b, 512 * b + 512)
+        add("pool", lambda q: q.affine_select(out[0], T.ones[:], [[-1, 512]], ALU.is_equal, 0.0, b, 4), [A("ones")], [out])
+
+    def dma(queue, out, in_, r, w):
+        add(queue, lambda q: q.dma_start(out, in_), r, w, "dma")
+
+    def send(t, hi, which):
+        dst = T.cores[rank ^ STEP[t]]
+        rel = relays(T, topo, core, dst)
+        ps = [pieces(t, hi)[k] for k in which]
+        if len(ps) > 1:
+            trs = []
+            for i, (k, name, a, b, sem, codes) in enumerate(ps):
+                eng = topo.engines(core, rel[k])
+                n = len(eng) // len(ps)
+                rid, pid = topo.addr(rel[k], core)
+                trs.append(RemoteDMATransfer(dst_ids=[DstId(rid=rid, pnc=pid)], dma_engine_mask=_mask(eng[n * i:n * i + n]),
+                                             remote_sem=T.sem[sem], src=view(T, name, a, codes), dst=view(T, name, b, codes)))
+                left[0] += n
+            add("pool", lambda q: q.remote_dma_fused(trs, local_sem=T.sem.left), [A(p[1], p[2][0], p[2][1]) for p in ps], [], "send")
+        else:
+            k, name, a, b, sem, codes = ps[0]
+            rid, pid = topo.addr(rel[k], core)
+            left[0] += len(topo.engines(core, rel[k]))
+            add("pool", lambda q: q.remote_dma(view(T, name, b, codes), view(T, name, a, codes), T.sem[sem], T.sem.left, pid, rid,
+                                               topo.mask(core, rel[k])), [A(name, a[0], a[1])], [], "send")
+
+    def arrive(t, hi, which):
+        src = T.cores[rank ^ STEP[t]]
+        rel = relays(T, topo, src, core)
+        ps = [pieces(t, 1 - hi)[k] for k in which]
+        ops.append({"q": None, "kind": "arrive", "r": [], "w": [(p[1], p[3][0], p[3][1], 1) for p in ps], "sem": ps[0][4],
+                    "val": sum(len(topo.engines(rel[p[0]], core)) for p in ps)})
+
+    def wrap(tmp, n, src):
+        scan(A(tmp[0], tmp[1], tmp[1] + n), A("cx", 0, n), src, 0.0, ALU.mult, ALU.add)
+
+    def unwrap(out, tmp, n, plus):
+        ts(out, A(tmp[0], tmp[1] + 15, tmp[1] + n, 16), A("scl", 0, 1), ALU.mult, float(plus), ALU.add)
+
+    dma("sync", T.x0[:], T.x[:], [], [A("x0")])
+    dma("scalar", T.ub[:], T.u[:], [], [A("ub")])
+    dma("sync", T.wq[:].bitcast(dt.uint8), T.wc[:], [A("x0")], [A("wq")])
+    dma("sync", T.wsc[:], T.ws[:], [], [A("wsc")])
+    dma("sync", T.vb[:], T.v[:], [], [A("vb")])
+    iota(A("pcol", 0, 1), [[0, 1]], 0, 1, False)
+    iota(A("offi"), [[8, 2], [16, 8]], 0, 0, False)
+    iota(A("t16"), [[0, 32], [1, 16]], 0, 0)
+    iota(A("iotaj"), [[1, 512]], -C, 0)
+    memset(A("ones"), 1.0)
+    ts(A("rcol", 0, 1), A("pcol", 0, 1), 15, ALU.bitwise_and)
+    copy(A("offu"), A("offi"))
+    memset(A("accg"), 0.0)
+    memset(A("fl"), 0.0)
+    copy(A("rf", 0, 1), A("rcol", 0, 1))
+    memset(A("wn"), -1024.0)
+    memset(A("invs"), 0.0)
+    ts(A("rf1", 0, 1), A("rf", 0, 1), 1.0, ALU.add)
+    ts(A("scl", 0, 1), A("rf", 0, 1), 15.0, ALU.is_equal, 1.0 / BIG, ALU.max)
+    ts(A("maskd", 0, C), A("t16", 0, C), A("rf", 0, 1), ALU.is_equal)
+    ts(A("c0", 0, C), A("t16", 0, C), 0.0, ALU.not_equal)
+    ts(A("ceq"), A("t16"), A("rf", 0, 1), ALU.not_equal)
+    ts(A("ctmp"), A("t16", 0, 16), A("rf1", 0, 1), ALU.is_equal, BIG, ALU.mult)
+    quant(A("uq"), A("us"), A("ub"))
+    add("vector", lambda q: q.tensor_copy(T.upq[:, 0:256].bitcast(dt.uint32), T.uq[:, 0:128].bitcast(dt.uint32).indirect(T.offu[:, 0:16])),
+        [A("uq"), A("offu")], [A("upq")])
+    add("scalar", lambda q: q.activation(T.ups[:, 0:256], T.us[:, 0:128].indirect(T.offu[:, 0:16]), ACT.Copy),
+        [A("us"), A("offu")], [A("ups")])
+    tt(A("cx", 0, 16), A("ctmp"), A("ceq", 0, 16), ALU.add)
+    act(A("iotak"), A("iotaj"), ACT.Copy)
+    for k in range(5):
+        act(A("cx", 16 << k, 32 << k), A("cx", 0, 16 << k), ACT.Copy)
+
+    for t in range(ROUNDS):
+        hi = 1 if rank & STEP[t] else 0
+        last = t == ROUNDS - 1
+        oo, po = C * hi, C * (1 - hi)
+        tq, tsc, msg, lb = "tq%d" % t, "ts%d" % t, "msg%d" % t, "lb%d" % t
+        ra_own, ra_par = A(msg, 16 * hi, 16 * hi + 16), A(msg, 16 * (1 - hi), 16 * (1 - hi) + 16)
+
+        quant(A(tq, 0, C), A(tsc, 0, C), A("x0" if t == 0 else "xn"))
+        send(t, hi, [0, 1])
+        send(t, hi, [2])
+        mm(1, "upq", "ups", 128, tq, tsc, 0, C)
+        mm(0, "upq", "ups", 0, tq, tsc, 0, C)
+        mm(2, "upq", "ups", 128, tq, tsc, 0, C)
+        if t == 0:
+            iota(A("klo"), [[16, 16]], 16 - C, 0)
+            iota(A("cw0"), [[16, 16]], 2 * C, 0, False)
+            for b in range(3):
+                unit(b)
+        tt(A("sm", 0, 64), A("p1", 0, 64), A("maskd", 0, 64), ALU.mult)
+        tt(A("sm", 64, C), A("p1", 64, C), A("maskd", 64, C), ALU.mult)
+        scan(A("sc", 0, 64), A("c0", 0, 64), A("sm", 0, 64), 0.0, ALU.mult, ALU.add)
+        tt(A("sm", C, 2 * C), A("p0", 0, C), A("maskd", 0, C), ALU.mult)
+        scan(A("sc", 64, C), A("c0", 64, C), A("sm", 64, C), 0.0, ALU.mult, ALU.add)
+        scan(A("sc", C, 2 * C), A("c0", 0, C), A("sm", C, 2 * C), 0.0, ALU.mult, ALU.add)
+        tt(A("eqf", 0, C), A("p1", 0, C), A("sc", 0, C), ALU.is_equal)
+        tt(A("eqf", C, 2 * C), A("p0", 0, C), A("sc", C, 2 * C), ALU.is_equal)
+
+        def compare(flags, bank, base, c):
+            s = A("sc", base + 16 * c + 15, base + 16 * c + 16)
+            e = 16 * c + 16
+            ts(A(flags, C * c, C * c + e), A(bank, 0, e), s, ALU.is_ge)
+            if e < C:
+                ts(A(flags, C * c + e, C * c + C), A(bank, e, C), s, ALU.is_gt)
+
+        def total(out, flags, c, init):
+            scan(A(out, 128 * c, 128 * c + 128), A(flags, C * c, C * c + 128), A(flags, C * c + 128, C * c + C), init, ALU.add, ALU.add)
+
+        for c in range(OWN_S):
+            act(A("sg", C * c, C * c + C), A("p2", 0, C), ACT.Sign, bias=A("sc", 16 * c + 15, 16 * c + 16), scale=-1.0)
+        for c in range(OWN_S):
+            e = 16 * c + 16
+            act(A("sg", C * c, C * c + e), A("sg", C * c, C * c + e), ACT.Relu, accum=A("accl", c, c + 1))
+            if e < C:
+                act(A("sg", C * c + e, C * c + C), A("sg", C * c + e, C * c + C), ACT.Relu, scale=-1.0, accum=A("accg", c, c + 1))
+
+        for c in range(16):
+            compare("fa", "p0", C, c)
+            if c == 1:
+                scan(A("eqs"), A("ceq"), A("eqf"), 0.0, ALU.mult, ALU.subtract)
+        for c in range(16):
+            total("sa", "fa", c, A("eqs", C + 16 * c + 15, C + 16 * c + 16))
+        if t == 0:
+            if OWN_S < 16:
+                memset(A("klo", OWN_S, 16), float(-C))
+            copy(A("khi", CROSS_S, 16), A("klo", CROSS_S, 16))
+            ts(A("khi", 0, CROSS_S), A("klo", 0, CROSS_S), float(C), ALU.add)
+        else:
+            tt(A("ke"), A("eqs", 15, C, 16), A("khi" if hi else "klo"), ALU.add)
+        ts(ra_own, A("sa", 127, 2048, 128), float(oo), ALU.add)
+        send(t, hi, [3])
+        if t == 0:
+            unit(3)
+            iota(A("nodet"), [[0, 2], [1, 128], [0, 2]], 0, 0)
+            tt(A("ke"), A("eqs", 15, C, 16), A("khi" if hi else "klo"), ALU.add)
+        for c in range(OWN_S, 16):
+            compare("fo", "p1", 0, c)
+        arrive(t, hi, [0, 1])
+        arrive(t, hi, [2])
+        mm(3, "upq", "ups", 128, tq, tsc, C, C)
+        mm(4, "upq", "ups", 128, tq, tsc, C, C)
+        cross = ALU.is_ge if hi else ALU.is_gt
+
+        for c in range(CROSS_S):
+            act(A("sgx", C * c, C * c + C), A("p4", 0, C), ACT.Sign, bias=A("sc", 16 * c + 15, 16 * c + 16), scale=-1.0)
+        for c in range(CROSS_S):
+            act(A("sgx", C * c, C * c + C), A("sgx", C * c, C * c + C), ACT.Relu, scale=1.0 if hi else -1.0, accum=A("accx", c, c + 1))
+        for c in range(OWN_S, 16):
+            total("so", "fo", c, A("ke", c, c + 1))
+
+        def against(c):
+            ts(A("fb", C * c, C * c + C), A("p3", 0, C), A("sc", 16 * c + 15, 16 * c + 16), cross)
+
+        def place(c):
+            total("sx", "fb", c, A("own", c, c + 1) if c < OWN_S else A("so", 128 * c + 127, 128 * c + 128))
+
+        for c in range(8, 16):
+            against(c)
+        tt(A("dd", 0, OWN_S), A("accg", 0, OWN_S), A("accl", 0, OWN_S), ALU.subtract)
+        against(7)
+        tt(A("own", 0, OWN_S), A("dd", 0, OWN_S), A("ke", 0, OWN_S), ALU.add)
+        against(6)
+        for c in range(8, 16):
+            place(c)
+        against(5)
+        ts(A(lb, 16 * hi + 8, 16 * hi + 16), A("sx", 128 * 8 + 127, 2048, 128), float(C), ALU.add)
+        send(t, hi, [4])
+        for c in range(CROSS_S, 5):
+            against(c)
+        for c in range(7, CROSS_S - 1, -1):
+            place(c)
+            if c == CROSS_S + 1:
+                tt(A("rbm", 0, CROSS_S), A("own", 0, CROSS_S), A("accx", 0, CROSS_S), ALU.subtract if hi else ALU.add)
+        ts(A(lb, 16 * hi, 16 * hi + CROSS_S), A("rbm", 0, CROSS_S), float(C), ALU.add)
+        ts(A(lb, 16 * hi + CROSS_S, 16 * hi + 8), A("sx", 128 * CROSS_S + 127, 1024, 128), float(C), ALU.add)
+        send(t, hi, [5])
+
+        def mates_a(lst, o):
+            scatter(A("inva", 0, o + C), lst, A("iotaj", o, o + C))
+            copy(A("invs", o, o + C, 2), A("inva", o + 1, o + C, 2))
+            copy(A("invs", o + 1, o + C, 2), A("inva", o, o + C, 2))
+
+        if t == 0:
+            quant(A("eq4"), A("es"), A("eb"))
+        mates_a(ra_own, oo)
+        banks = [5, 6, 7, 0]
+        for b in range(4):
+            mm(banks[b], "eq4", "es", 128 * b, tq, tsc, 0, 2 * C)
+        for b in range(4):
+            act(A("dpp", C * b, C * b + C), A("p%d" % banks[b], C, 2 * C), ACT.Copy, scale=0.5)
+        act(A("arep", oo, oo + C), G(A("invs", 0, oo + C), ra_own), ACT.Copy)
+        arrive(t, hi, [3])
+        mates_a(ra_par, po)
+        wrap(("xs", 0), 128, A("inva", po, po + C, 2))
+        wrap(("xs", 128), 128, A("inva", po + 1, po + C, 2))
+        act(A("dp", 0, C), A("p%d" % banks[0], 0, C), ACT.Copy)
+        act(A("arep", po, po + C), G(A("invs", 0, po + C), ra_par), ACT.Copy)
+        if t == 0:
+            ts(A("cw"), A("cw0"), A("rf", 0, 1), ALU.add)
+        unwrap(A("evl"), ("xs", 0), C, C - po)
+        scatter(A("mm"), A(lb, 16 * hi, 16 * hi + 16), A("arep", oo, oo + C))
+        for b in range(4):
+            act(A("g1", 128 * b, 128 * b + 128), G(A("dpp", C * b, C * b + C), A("evl", 0, 8)), ACT.Copy)
+        if t == 1:
+            quant(A("vq"), A("vs"), A("vb"))
+        for b in range(4):
+            tt(A("bt", b, 512, 4), G(A("dpp", C * b, C * b + C), A("evl", 8, 16)), A("g1", 128 * b, 128 * b + 128), ALU.add)
+        arrive(t, hi, [4])
+        scatter(A("mm"), A(lb, 16 * (1 - hi) + 8, 16 * (1 - hi) + 16), A("arep", po + 128, po + C))
+        quant(A("bq"), A("bs"), A("bt"))
+        for b in range(4):
+            mm(1 + b, "eq4", "es", 128 * b, "bq", "bs", 0, 128)
+        for b in range(1, 4):
+            act(A("dp", 384 * b, 384 * b + C), A("p%d" % banks[b], 0, C), ACT.Copy)
+
+        arrive(t, hi, [5])
+        scatter(A("mm"), A(lb, 16 * (1 - hi), 16 * (1 - hi) + 8), A("arep", po, po + 128))
+        copy(A("ms", 0, 512, 2), A("mm", 1, 512, 2))
+        copy(A("ms", 1, 512, 2), A("mm", 0, 512, 2))
+        act(A("pa", C, 2 * C), G(A("ms"), A(lb, 16, 32)), ACT.Copy)
+        copy(A("pa", 0, C), G(A("ms"), A(lb, 0, 16)))
+        wrap(("xs", 0), C, A("pa", 0, C))
+        wrap(("xs", C), C, A("pa", C, 2 * C))
+        unwrap(A("ll", 0, 32), ("xs", 0), 512, C)
+        P, low = ["pa", "pb"], ["lowa", "lowb"]
+        for k in range(DOUBLINGS):
+            lst = A("ll", 32 * k, 32 * k + 32)
+            new = low[(k + 1) % 2]
+            if k < DOUBLINGS - 1:
+                act(A(P[(k + 1) % 2]), G(A(P[k % 2]), lst), ACT.Copy)
+                if k == 0:
+                    tt(A(new), G(A("iotaj"), lst), A("iotak"), ALU.min)
+                else:
+                    tt(A(new), G(A(low[k % 2]), lst), A("lowc"), ALU.min)
+                act(A("lowc", 0, 384), A(new, 0, 384), ACT.Copy)
+                tmp = "xs" if k % 2 else "xs2"
+                wrap((tmp, 0), 512, A(P[(k + 1) % 2]))
+                copy(A("lowc", 384, 512), A(new, 384, 512))
+                unwrap(A("ll", 32 * k + 32, 32 * k + 64), (tmp, 0), 512, C)
+                if k < 4:
+                    wrap(("xs3", 128 * k), 128, A("arep", 128 * k, 128 * k + 128))
+                elif k == 4:
+                    unwrap(A("awl"), ("xs3", 0), 512, C)
+            else:
+                for h in (1 - hi, hi):
+                    tt(A(new, C * h, C * h + C), G(A(low[k % 2]), A("ll", 32 * k + 16 * h, 32 * k + 16 * h + 16)), A("lowc", C * h, C * h + C), ALU.min)
+                    act(A("pa", C * h, C * h + C), A(new, C * h, C * h + C), ACT.Copy)
+        act(A("nodep"), G(A("nodet"), ra_par), ACT.Copy)
+        for b in range(4):
+            act(A("dp", 384 * b + C, 384 * b + 384), A("p%d" % (1 + b), 0, 128), ACT.Copy)
+
+        lw = low[DOUBLINGS % 2]
+        for h in (1 - hi, hi):
+            tt(A("fl", 16 + 272 * h, 272 + 272 * h), G(A(lw, 0, C * h + C), A("awl", 16 * h, 16 * h + 16)), A("pa", C * h, C * h + C), ALU.is_gt)
+        for h in (1 - hi, hi):
+            scan(A("vv", C * h, C * h + C), A("fl", 16 + 272 * h, 272 + 272 * h), A("fl", 15 + 272 * h, 271 + 272 * h), 0.0, ALU.add, ALU.add)
+        wrap(("xs", 0), C, A("vv", po, po + C))
+        wrap(("xs", C), C, A("vv", oo, oo + C))
+        unwrap(A("wi", 0, 16), ("xs", 0), C, 1)
+        unwrap(A("lu", 16, 32), ("xs", C), C, 1)
+        ts(A("nf", 0, 16), A("wi", 0, 16), 1, ALU.bitwise_and)
+        if last:
+            unwrap(A("wi", 16, 32), ("xs", C), C, 1)
+        tt(A("tc", 0, 16), A("nf", 0, 16), A("cw"), ALU.mult)
+        if last:
+            ts(A("nf", 16, 32), A("wi", 16, 32), 1, ALU.bitwise_and)
+        tt(A("lm", 0, 16), A("tc", 0, 16), A("wi", 0, 16), ALU.max)
+        if last:
+            ts(A("hh", 16, 32), A("wi", 16, 32), 1, ALU.arith_shift_right)
+        copy(A("lu", 0, 16), A("lm", 0, 16))
+        if last:
+            tt(A("tc", 16, 32), A("nf", 16, 32), A("cw"), ALU.mult)
+        scatter(A("wn"), A("lu", 0, 16), A("nodep"))
+        if last:
+            tt(A("lm", 16, 32), A("tc", 16, 32), A("hh", 16, 32), ALU.max)
+        tt(A("yv"), G(A("wn"), A("lu", 16, 32)), A("iotaj", 0, C), ALU.max)
+        if last:
+            copy(A("ol16"), A("lm", 16, 32))
+        wrap(("xs2", 0), C, A("yv"))
+        unwrap(A("yl"), ("xs2", 0), C, C)
+
+        H = C // HALVES
+        for h in range(HALVES):
+            for b in range(4):
+                win = G(A("dp", 384 * b, 384 * b + 384), A("yl", H // 16 * h, H // 16 * (h + 1)))
+                if b % 2:
+                    act(A("yt", 4 * H * h + b, 4 * H * (h + 1), 4), win, ACT.Copy)
+                else:
+                    copy(A("yt", 4 * H * h + b, 4 * H * (h + 1), 4), win)
+            quant(A("zq", H * h, H * h + H), A("zs", H * h, H * h + H), A("yt", 4 * H * h, 4 * H * (h + 1)))
+        for h in range(HALVES):
+            for b in (0, 1, 4, 2, 5, 3, 6, 7):
+                mm(b, "wq" if b < 4 else "eq4", "wsc" if b < 4 else "es", 128 * (b % 4), "zq", "zs", H * h, H)
+            for b in range(4):
+                act(A("rr", C * b + H * h, C * b + H * h + H), A("p%d" % b, 0, H), ACT.Relu, scale=0.03125)
+                tt(A("xn", 4 * H * h + b, 4 * H * (h + 1), 4), A("p%d" % (4 + b), 0, H), A("rr", C * b + H * h, C * b + H * h + H), ALU.add)
+
+    tq, tsc = "tq%d" % ROUNDS, "ts%d" % ROUNDS
+
+    def scales(queue, k):
+        dma(queue, T.osc[4 * k:4 * k + 4, :], T[tsc][32 * k:32 * k + 4, 0:C], [A(tsc)], [])
+
+    quant(A(tq), A(tsc), A("xn"))
+    mm(0, "vq", "vs", 0, tq, tsc, 0, C)
+    dma("sync", T.oc[:, :], T[tq][:, 0:C].bitcast(dt.uint8), [A(tq)], [])
+    scatter(A("wo"), A("ol16"), A("iotaj", C, 2 * C))
+    scales("sync", 0)
+    scales("scalar", 1)
+    scales("sync", 2)
+    act(A("yo"), A("p0", 0, C), ACT.Copy)
+    dma("scalar", T.y[:, :], T.yo[:], [A("yo")], [])
+    scales("scalar", 3)
+    dma("sync", T.ol[:, :], T.wo[0:128:16, 1:129], [A("wo")], [])
+    emit(g, T, ops, left[0])

@@ -16,13 +16,14 @@ Q4, U8, BF, F32, I32, U16 = "float8_e4m3fn_x4", "uint8", "bfloat16", "float32", 
 SCRATCH = {}
 for _d, _l in [
     (BF, "x0 1024 xn 1024 ub 512 vb 512 ones 512 eb 2048 t16 512 maskd 512 ceq 512 c0 512 cx 512 ctmp 16 iotaj 512 iotak 512 "
-         "nodet 512 wn 768 eqf 512 eqs 512 fa 4096 fb 4096 fo 4096 sa 2048 so 2048 sx 2048 sg 4096 sgx 4096 inva 512 invs 512 "
+         "nodet 512 wn 784 eqf 512 eqs 512 fa 4096 fb 4096 fo 4096 sa 2048 so 2048 sx 2048 sg 4096 sgx 4096 inva 512 invs 512 "
          "arep 512 xs 512 xs2 512 xs3 512 mm 512 ms 512 pa 512 pb 512 lowa 512 lowb 512 lowc 512 fl 544 vv 512 nodep 256 yv 256 "
          "dp 1536 dpp 1024 g1 512 bt 512 yt 1024"),
     (Q4, "uq 128 upq 256 vq 128 wq 512 eq4 512 bq 128 zq 256 tq0 512 tq1 512 tq2 512 tq3 256"),
     (U8, "us 128 ups 256 vs 128 wsc 512 es 512 bs 128 zs 256 ts0 512 ts1 512 ts2 512 ts3 256"),
     (I32, "pcol 8 rcol 8 offi 16 cw0 16 cw 16 wi 32 hh 32 nf 32 tc 32 lm 32"),
-    (F32, "rf 8 rf1 8 scl 8 klo 16 khi 16 wo 768 sm 512 sc 512 accl 16 accg 16 accx 16 ke 16 dd 16 own 16 rbm 16 rr 1024 yo 256"),
+    (F32, "rf 8 rf1 8 scl 8 klo 16 khi 16 wo 768 sm 512 sc 512 accl 16 accg 16 accx 16 ke 16 dd 16 own 16 rbm 16 rr 1024 yo 256 "
+          "tf 16 tg 16 wf 16 lf 16 cf 16"),
     (U16, "offu 16 evl 16 awl 32 ll 256 lu 32 yl 16 ol16 16 msg0 32 msg1 32 msg2 32 lb0 32 lb1 32 lb2 32"),
 ]:
     _w = _l.split()
@@ -124,7 +125,11 @@ def emit(g, T, ops, left):
             if waited[o["q"]].get(key, -1) >= pos:
                 continue
             if key == o["q"] and o["kind"] == "c":
-                pos = max(pos, o["pos"] - 2)
+                k, span = o["pos"] - 1, 0
+                while k > pos and span < 600:
+                    span += sum(max(64, (r[2] - r[1]) // r[3] // 2) for r in ops[lines[key][k]]["w"][:1])
+                    k -= 1
+                pos = k
             waited[o["q"]][key] = pos
             j = key[1] if isinstance(key, tuple) else lines[key][pos]
             ops[j]["inc"] = True
@@ -279,7 +284,6 @@ def rank_program(g, core, T, topo):
     memset(A("fl"), 0.0)
     copy(A("rf", 0, 1), A("rcol", 0, 1))
     memset(A("wn"), -1024.0)
-    memset(A("invs"), 0.0)
     ts(A("rf1", 0, 1), A("rf", 0, 1), 1.0, ALU.add)
     ts(A("scl", 0, 1), A("rf", 0, 1), 15.0, ALU.is_equal, 1.0 / BIG, ALU.max)
     ts(A("maskd", 0, C), A("t16", 0, C), A("rf", 0, 1), ALU.is_equal)
@@ -316,8 +320,8 @@ def rank_program(g, core, T, topo):
                 unit(b)
         tt(A("sm", 0, 64), A("p1", 0, 64), A("maskd", 0, 64), ALU.mult)
         tt(A("sm", 64, C), A("p1", 64, C), A("maskd", 64, C), ALU.mult)
-        scan(A("sc", 0, 64), A("c0", 0, 64), A("sm", 0, 64), 0.0, ALU.mult, ALU.add)
         tt(A("sm", C, 2 * C), A("p0", 0, C), A("maskd", 0, C), ALU.mult)
+        scan(A("sc", 0, 64), A("c0", 0, 64), A("sm", 0, 64), 0.0, ALU.mult, ALU.add)
         scan(A("sc", 64, C), A("c0", 64, C), A("sm", 64, C), 0.0, ALU.mult, ALU.add)
         scan(A("sc", C, 2 * C), A("c0", 0, C), A("sm", C, 2 * C), 0.0, ALU.mult, ALU.add)
         tt(A("eqf", 0, C), A("p1", 0, C), A("sc", 0, C), ALU.is_equal)
@@ -402,35 +406,35 @@ def rank_program(g, core, T, topo):
         ts(A(lb, 16 * hi + CROSS_S, 16 * hi + 8), A("sx", 128 * CROSS_S + 127, 1024, 128), float(C), ALU.add)
         send(t, hi, [5])
 
-        def mates_a(lst, o):
-            scatter(A("inva", 0, o + C), lst, A("iotaj", o, o + C))
-            copy(A("invs", o, o + C, 2), A("inva", o + 1, o + C, 2))
-            copy(A("invs", o + 1, o + C, 2), A("inva", o, o + C, 2))
-
+        scatter(A("inva", 0, oo + C), ra_own, A("iotaj", oo, oo + C))
         if t == 0:
             quant(A("eq4"), A("es"), A("eb"))
-        mates_a(ra_own, oo)
         banks = [5, 6, 7, 0]
         for b in range(4):
             mm(banks[b], "eq4", "es", 128 * b, tq, tsc, 0, 2 * C)
         for b in range(4):
             act(A("dpp", C * b, C * b + C), A("p%d" % banks[b], C, 2 * C), ACT.Copy, scale=0.5)
-        act(A("arep", oo, oo + C), G(A("invs", 0, oo + C), ra_own), ACT.Copy)
         arrive(t, hi, [3])
-        mates_a(ra_par, po)
-        wrap(("xs", 0), 128, A("inva", po, po + C, 2))
-        wrap(("xs", 128), 128, A("inva", po + 1, po + C, 2))
+        scatter(A("inva", 0, po + C), ra_par, A("iotaj", po, po + C))
         act(A("dp", 0, C), A("p%d" % banks[0], 0, C), ACT.Copy)
-        act(A("arep", po, po + C), G(A("invs", 0, po + C), ra_par), ACT.Copy)
         if t == 0:
             ts(A("cw"), A("cw0"), A("rf", 0, 1), ALU.add)
+            ts(A("cf"), A("cw0"), A("rf", 0, 1), ALU.add, float(-2 * C), ALU.add)
+        wrap(("xs", 0), 128, A("inva", po, po + C, 2))
+        wrap(("xs", 128), 128, A("inva", po + 1, po + C, 2))
+        copy(A("invs", 0, 2 * C, 2), A("inva", 1, 2 * C, 2))
+        copy(A("invs", 1, 2 * C, 2), A("inva", 0, 2 * C, 2))
         unwrap(A("evl"), ("xs", 0), C, C - po)
-        scatter(A("mm"), A(lb, 16 * hi, 16 * hi + 16), A("arep", oo, oo + C))
+        copy(A("arep", oo, oo + C), G(A("invs"), ra_own))
         for b in range(4):
             act(A("g1", 128 * b, 128 * b + 128), G(A("dpp", C * b, C * b + C), A("evl", 0, 8)), ACT.Copy)
+            if b == 1:
+                act(A("arep", po, po + C), G(A("invs"), ra_par), ACT.Copy)
+        tt(A("bt", 0, 512, 4), G(A("dpp", 0, C), A("evl", 8, 16)), A("g1", 0, 128), ALU.add)
+        scatter(A("mm"), A(lb, 16 * hi, 16 * hi + 16), A("arep", oo, oo + C))
         if t == 1:
             quant(A("vq"), A("vs"), A("vb"))
-        for b in range(4):
+        for b in range(1, 4):
             tt(A("bt", b, 512, 4), G(A("dpp", C * b, C * b + C), A("evl", 8, 16)), A("g1", 128 * b, 128 * b + 128), ALU.add)
         arrive(t, hi, [4])
         scatter(A("mm"), A(lb, 16 * (1 - hi) + 8, 16 * (1 - hi) + 16), A("arep", po + 128, po + C))
@@ -446,65 +450,89 @@ def rank_program(g, core, T, topo):
         copy(A("ms", 1, 512, 2), A("mm", 0, 512, 2))
         act(A("pa", C, 2 * C), G(A("ms"), A(lb, 16, 32)), ACT.Copy)
         copy(A("pa", 0, C), G(A("ms"), A(lb, 0, 16)))
-        wrap(("xs", 0), C, A("pa", 0, C))
-        wrap(("xs", C), C, A("pa", C, 2 * C))
-        unwrap(A("ll", 0, 32), ("xs", 0), 512, C)
         P, low = ["pa", "pb"], ["lowa", "lowb"]
-        for k in range(DOUBLINGS):
-            lst = A("ll", 32 * k, 32 * k + 32)
-            new = low[(k + 1) % 2]
-            if k < DOUBLINGS - 1:
-                act(A(P[(k + 1) % 2]), G(A(P[k % 2]), lst), ACT.Copy)
-                if k == 0:
-                    tt(A(new), G(A("iotaj"), lst), A("iotak"), ALU.min)
-                else:
-                    tt(A(new), G(A(low[k % 2]), lst), A("lowc"), ALU.min)
-                act(A("lowc", 0, 384), A(new, 0, 384), ACT.Copy)
-                tmp = "xs" if k % 2 else "xs2"
-                wrap((tmp, 0), 512, A(P[(k + 1) % 2]))
-                copy(A("lowc", 384, 512), A(new, 384, 512))
-                unwrap(A("ll", 32 * k + 32, 32 * k + 64), (tmp, 0), 512, C)
-                if k < 4:
-                    wrap(("xs3", 128 * k), 128, A("arep", 128 * k, 128 * k + 128))
-                elif k == 4:
-                    unwrap(A("awl"), ("xs3", 0), 512, C)
+
+        def listed(k, h, step):
+            tmp = ("xs" if k % 2 else "xs2", C * h)
+            if step == 0:
+                wrap(tmp, C, A(P[k % 2], C * h, C * h + C))
             else:
-                for h in (1 - hi, hi):
-                    tt(A(new, C * h, C * h + C), G(A(low[k % 2]), A("ll", 32 * k + 16 * h, 32 * k + 16 * h + 16)), A("lowc", C * h, C * h + C), ALU.min)
-                    act(A("pa", C * h, C * h + C), A(new, C * h, C * h + C), ACT.Copy)
+                unwrap(A("ll", 32 * k + 16 * h, 32 * k + 16 * h + 16), tmp, C, C)
+
+        def least(k, a, b):
+            win, other = (A("iotaj"), "iotak") if k == 0 else (A(low[k % 2]), "lowc")
+            tt(A(low[(k + 1) % 2], a, b), G(win, A("ll", 32 * k + a // 16, 32 * k + b // 16)), A(other, a, b), ALU.min)
+
+        def again(k, a, b, to="lowc"):
+            act(A(to, a, b), A(low[(k + 1) % 2], a, b), ACT.Copy)
+
+        listed(0, 0, 0)
+        listed(0, 1, 0)
+        listed(0, 0, 1)
+        listed(0, 1, 1)
+        for k in range(DOUBLINGS - 1):
+            for h in range(2):
+                act(A(P[(k + 1) % 2], C * h, C * h + C), G(A(P[k % 2]), A("ll", 32 * k + 16 * h, 32 * k + 16 * h + 16)), ACT.Copy)
+            if k > 0:
+                again(k - 1, 384, 512)
+            least(k, 0, C)
+            again(k, 0, C)
+            listed(k + 1, 0, 0)
+            least(k, C, 384)
+            listed(k + 1, 0, 1)
+            listed(k + 1, 1, 0)
+            least(k, 384, 512)
+            again(k, C, 384)
+            listed(k + 1, 1, 1)
+            if k < 4:
+                wrap(("xs3", 128 * k), 128, A("arep", 128 * k, 128 * k + 128))
+            elif k == 4:
+                unwrap(A("awl"), ("xs3", 0), 512, C)
+        k = DOUBLINGS - 1
+        again(k - 1, 384, 512)
+        for h in (1 - hi, hi):
+            least(k, C * h, C * h + C)
+            again(k, C * h, C * h + C, "pa")
         act(A("nodep"), G(A("nodet"), ra_par), ACT.Copy)
         for b in range(4):
             act(A("dp", 384 * b + C, 384 * b + 384), A("p%d" % (1 + b), 0, 128), ACT.Copy)
 
         lw = low[DOUBLINGS % 2]
+
+        def fl(h, shift):
+            return A("fl", 16 + 272 * h - shift, 272 + 272 * h - shift)
+
         for h in (1 - hi, hi):
-            tt(A("fl", 16 + 272 * h, 272 + 272 * h), G(A(lw, 0, C * h + C), A("awl", 16 * h, 16 * h + 16)), A("pa", C * h, C * h + C), ALU.is_gt)
-        for h in (1 - hi, hi):
-            scan(A("vv", C * h, C * h + C), A("fl", 16 + 272 * h, 272 + 272 * h), A("fl", 15 + 272 * h, 271 + 272 * h), 0.0, ALU.add, ALU.add)
+            tt(fl(h, 0), G(A(lw, 0, C * h + C), A("awl", 16 * h, 16 * h + 16)), A("pa", C * h, C * h + C), ALU.is_gt)
+        scan(A("vv", po, po + C), fl(1 - hi, 0), fl(1 - hi, 1), 0.0, ALU.add, ALU.add)
+        wrap(("xs2", 0), C, fl(1 - hi, 0))
+        scan(A("vv", oo, oo + C), fl(hi, 0), fl(hi, 1), 0.0, ALU.add, ALU.add)
         wrap(("xs", 0), C, A("vv", po, po + C))
+        ts(A("tf"), A("xs2", 15, C, 16), A("scl", 0, 1), ALU.mult, 1024.0, ALU.mult)
         wrap(("xs", C), C, A("vv", oo, oo + C))
-        unwrap(A("wi", 0, 16), ("xs", 0), C, 1)
-        unwrap(A("lu", 16, 32), ("xs", C), C, 1)
-        ts(A("nf", 0, 16), A("wi", 0, 16), 1, ALU.bitwise_and)
+        unwrap(A("wf"), ("xs", 0), C, 513)
+        tt(A("tg"), A("tf"), A("cf"), ALU.add)
+        unwrap(A("lu", 16, 32), ("xs", C), C, 513)
+        tt(A("lf"), A("tg"), A("wf"), ALU.min)
         if last:
             unwrap(A("wi", 16, 32), ("xs", C), C, 1)
-        tt(A("tc", 0, 16), A("nf", 0, 16), A("cw"), ALU.mult)
+        copy(A("lu", 0, 16), A("lf"))
         if last:
             ts(A("nf", 16, 32), A("wi", 16, 32), 1, ALU.bitwise_and)
-        tt(A("lm", 0, 16), A("tc", 0, 16), A("wi", 0, 16), ALU.max)
-        if last:
             ts(A("hh", 16, 32), A("wi", 16, 32), 1, ALU.arith_shift_right)
-        copy(A("lu", 0, 16), A("lm", 0, 16))
-        if last:
-            tt(A("tc", 16, 32), A("nf", 16, 32), A("cw"), ALU.mult)
         scatter(A("wn"), A("lu", 0, 16), A("nodep"))
         if last:
+            tt(A("tc", 16, 32), A("nf", 16, 32), A("cw"), ALU.mult)
+        for h in range(2):
+            tt(A("yv", 128 * h, 128 * h + 128), G(A("wn"), A("lu", 16 + 8 * h, 24 + 8 * h)), A("iotaj", 128 * h, 128 * h + 128), ALU.max)
+        for h in range(2):
+            wrap(("xs2", 128 * h), 128, A("yv", 128 * h, 128 * h + 128))
+        if last:
             tt(A("lm", 16, 32), A("tc", 16, 32), A("hh", 16, 32), ALU.max)
-        tt(A("yv"), G(A("wn"), A("lu", 16, 32)), A("iotaj", 0, C), ALU.max)
+        for h in range(2):
+            unwrap(A("yl", 8 * h, 8 * h + 8), ("xs2", 128 * h), 128, C)
         if last:
             copy(A("ol16"), A("lm", 16, 32))
-        wrap(("xs2", 0), C, A("yv"))
-        unwrap(A("yl"), ("xs2", 0), C, C)
 
         H = C // HALVES
         for h in range(HALVES):

@@ -4,27 +4,26 @@ from concourse.mybir import dt, AluOpType, ActivationFunctionType
 ALU = AluOpType
 ACT = ActivationFunctionType
 C = 256
+H = C // 2
 ROUNDS = 3
 STEP = [1, 2, 4]
 DOUBLINGS = 8
-OWN_S = 16
-CROSS_S = 4
-HALVES = 2
+CROSS_S = 3
+SPLIT = 128
 BIG = 2.0 ** 40
 Q4, U8, BF, F32, I32, U16 = "float8_e4m3fn_x4", "uint8", "bfloat16", "float32", "int32", "uint16"
 
 SCRATCH = {}
 for _d, _l in [
-    (BF, "x0 1024 xn 1024 ub 512 vb 512 ones 512 eb 2048 t16 512 maskd 512 ceq 512 c0 512 cx 512 ctmp 16 iotaj 512 iotak 512 "
-         "nodet 512 wn 784 eqf 512 eqs 512 fa 4096 fb 4096 fo 4096 sa 2048 so 2048 sx 2048 sg 4096 sgx 4096 inva 512 invs 512 "
-         "arep 512 xs 512 xs2 512 xs3 512 mm 512 ms 512 pa 512 pb 512 lowa 512 lowb 512 lowc 512 fl 544 vv 512 nodep 256 yv 256 "
-         "dp 1536 dpp 1024 g1 512 bt 512 yt 1024"),
-    (Q4, "uq 128 upq 256 vq 128 wq 512 eq4 512 bq 128 zq 256 tq0 512 tq1 512 tq2 512 tq3 256"),
-    (U8, "us 128 ups 256 vs 128 wsc 512 es 512 bs 128 zs 256 ts0 512 ts1 512 ts2 512 ts3 256"),
-    (I32, "pcol 8 rcol 8 offi 16 cw0 16 cw 16 wi 32 hh 32 nf 32 tc 32 lm 32"),
-    (F32, "rf 8 rf1 8 scl 8 klo 16 khi 16 wo 768 sm 512 sc 512 accl 16 accg 16 accx 16 ke 16 dd 16 own 16 rbm 16 rr 1024 yo 256 "
-          "tf 16 tg 16 wf 16 lf 16 cf 16"),
-    (U16, "offu 16 evl 16 awl 32 ll 256 lu 32 yl 16 ol16 16 msg0 32 msg1 32 msg2 32 lb0 32 lb1 32 lb2 32"),
+    (BF, "x0 1024 xn 1024 ub 512 vb 512 ones 512 eb 2048 t16 512 maskd 128 ceq 512 c0 128 cx 256 ctmp 16 iotaj 512 "
+         "cx2 256 wn 272 eqf 512 eqs 512 fa 4096 fb 4096 sa 2048 sx 2048 sg 4096 sgx 4096 inva 512 inw 512 invs 512 "
+         "arep 512 xs 512 xs2 512 xs3 512 xs4 256 xs5 256 xs6 256 xs7 256 mm 512 ms 512 pa 512 pb 512 lowa 512 lowb 512 lowc 512 lowd 512 "
+         "fl 544 vv 256 fa1 256 fb1 272 sp 256 ge 256 yv 256 dp 1536 dpp 1024 g1 1024 bt 1024 alt 256 yt 1024"),
+    (Q4, "uq 128 upq 256 vq 128 wq 512 eq4 512 bq 256 zq 256 tq0 512 tq1 512 tq2 512 tq3 256"),
+    (U8, "us 128 ups 256 vs 128 wsc 512 es 512 bs 256 zs 256 ts0 512 ts1 512 ts2 512 ts3 256"),
+    (I32, "pcol 8 rcol 8 offi 16 cw0 16 cw 16 wi 16 hh 16 nf 16 tc 16 lm 16"),
+    (F32, "rf 8 rf1 8 scl 8 scl2 8 klo 16 khi 16 wo 768 sm 512 sc 512 accl 16 accg 16 accx 16 ke 16 dd 16 own 16 rbm 16 rr 1024 yo 256"),
+    (U16, "offu 16 inl 16 awl 32 ll 256 lu 16 kl 8 yl 16 ol16 16 msg0 32 msg1 32 msg2 32 lb0 32 lb1 32 lb2 32"),
 ]:
     _w = _l.split()
     for _i in range(0, len(_w), 2):
@@ -55,8 +54,8 @@ def pieces(t, hi):
     out = [(1 + k, "tq%d" % t, (128 * k, 128 * k + 128), (C + 128 * k, C + 128 * k + 128), "at%d" % t, True) for k in range(2)]
     out.append((3, "ts%d" % t, (0, C), (C, 2 * C), "as%d" % t, False))
     out.append((0, "msg%d" % t, (o, o + 16), (o, o + 16), "am%d" % t, False))
-    out.append((1, "lb%d" % t, (o + 8, o + 16), (o + 8, o + 16), "aq%d" % t, False))
-    out.append((0, "lb%d" % t, (o, o + 8), (o, o + 8), "ar%d" % t, False))
+    out.append((1, "lb%d" % t, (o, o + 8), (o, o + 8), "aq%d" % t, False))
+    out.append((0, "lb%d" % t, (o + 8, o + 16), (o + 8, o + 16), "ar%d" % t, False))
     return out
 
 
@@ -75,8 +74,7 @@ def relay_program(g, core, T, topo):
             for k, name, a, b, sem, codes in pieces(t, 1 if r & STEP[t] else 0):
                 if rel[k] != core:
                     continue
-                n = len(topo.engines(src, core))
-                g.wait_ge(T.sem[sem], n // 2 if codes else n)
+                g.wait_ge(T.sem[sem], len(topo.engines(src, core)))
                 rid, pid = topo.addr(dst, core)
                 g.remote_dma(view(T, name, b, codes), view(T, name, b, codes), T.sem[sem], T.sem.left, pid, rid, topo.mask(core, dst))
                 left += len(topo.engines(core, dst))
@@ -284,22 +282,56 @@ def rank_program(g, core, T, topo):
     memset(A("fl"), 0.0)
     copy(A("rf", 0, 1), A("rcol", 0, 1))
     memset(A("wn"), -1024.0)
+    memset(A("fb1", 0, 16), 0.0)
+    memset(A("cx2", 1, C, 2), 1.0)
+    memset(A("alt", 0, C, 2), 0.0)
+    memset(A("alt", 1, C, 2), 1.0)
     ts(A("rf1", 0, 1), A("rf", 0, 1), 1.0, ALU.add)
     ts(A("scl", 0, 1), A("rf", 0, 1), 15.0, ALU.is_equal, 1.0 / BIG, ALU.max)
-    ts(A("maskd", 0, C), A("t16", 0, C), A("rf", 0, 1), ALU.is_equal)
-    ts(A("c0", 0, C), A("t16", 0, C), 0.0, ALU.not_equal)
-    ts(A("ceq"), A("t16"), A("rf", 0, 1), ALU.not_equal)
+    ts(A("maskd"), A("t16", 0, H), A("rf", 0, 1), ALU.is_equal)
+    ts(A("c0"), A("t16", 0, H), 0.0, ALU.not_equal)
     ts(A("ctmp"), A("t16", 0, 16), A("rf1", 0, 1), ALU.is_equal, BIG, ALU.mult)
+    ts(A("scl2", 0, 1), A("scl", 0, 1), 2.0, ALU.mult)
     quant(A("uq"), A("us"), A("ub"))
+    ts(A("ceq"), A("t16"), A("rf", 0, 1), ALU.not_equal)
     add("vector", lambda q: q.tensor_copy(T.upq[:, 0:256].bitcast(dt.uint32), T.uq[:, 0:128].bitcast(dt.uint32).indirect(T.offu[:, 0:16])),
         [A("uq"), A("offu")], [A("upq")])
     add("scalar", lambda q: q.activation(T.ups[:, 0:256], T.us[:, 0:128].indirect(T.offu[:, 0:16]), ACT.Copy),
         [A("us"), A("offu")], [A("ups")])
     tt(A("cx", 0, 16), A("ctmp"), A("ceq", 0, 16), ALU.add)
-    act(A("iotak"), A("iotaj"), ACT.Copy)
-    for k in range(5):
-        act(A("cx", 16 << k, 32 << k), A("cx", 0, 16 << k), ACT.Copy)
+    quant(A("tq0", 0, C), A("ts0", 0, C), A("x0"))
 
+    def scores(t, h):
+        tq, tsc = "tq%d" % t, "ts%d" % t
+        mm((4, 5)[h], "upq", "ups", 128, tq, tsc, H * h, H)
+        mm((1, 6)[h], "upq", "ups", 128, tq, tsc, H * h, H)
+        mm((0, 2)[h], "upq", "ups", 0, tq, tsc, 0, H * h + H)
+
+    def half(k, h):
+        return A("p%d" % ((4, 5), (0, 2))[k][h], H * h * k, H * h * k + H)
+
+    def mask(k, h):
+        tt(A("sm", C * k + H * h, C * k + H * h + H), half(k, h), A("maskd"), ALU.mult)
+
+    def hold(k, h):
+        o = C * k + H * h
+        scan(A("sc", o, o + H), A("c0"), A("sm", o, o + H), 0.0, ALU.mult, ALU.add)
+
+    def equal(k, h):
+        o = C * k + H * h
+        tt(A("eqf", o, o + H), half(k, h), A("sc", o, o + H), ALU.is_equal)
+
+    def results(h):
+        tq, tsc = "tq%d" % ROUNDS, "ts%d" % ROUNDS
+        dma("sync", T.oc[:, 4 * H * h:4 * H * (h + 1)], T[tq][:, H * h:H * h + H].bitcast(dt.uint8), [A(tq, H * h, H * h + H)], [])
+        if h:
+            mm(0, "vq", "vs", 0, tq, tsc, 0, C)
+            act(A("yo"), A("p0", 0, C), ACT.Copy)
+            dma("scalar", T.y[:, :], T.yo[:], [A("yo")], [])
+
+    send(0, rank & STEP[0], [0])
+    scores(0, 0)
+    mask(0, 0)
     for t in range(ROUNDS):
         hi = 1 if rank & STEP[t] else 0
         last = t == ROUNDS - 1
@@ -307,263 +339,358 @@ def rank_program(g, core, T, topo):
         tq, tsc, msg, lb = "tq%d" % t, "ts%d" % t, "msg%d" % t, "lb%d" % t
         ra_own, ra_par = A(msg, 16 * hi, 16 * hi + 16), A(msg, 16 * (1 - hi), 16 * (1 - hi) + 16)
 
-        quant(A(tq, 0, C), A(tsc, 0, C), A("x0" if t == 0 else "xn"))
-        send(t, hi, [0, 1])
+        send(t, hi, [1])
         send(t, hi, [2])
-        mm(1, "upq", "ups", 128, tq, tsc, 0, C)
-        mm(0, "upq", "ups", 0, tq, tsc, 0, C)
-        mm(2, "upq", "ups", 128, tq, tsc, 0, C)
+        scores(t, 1)
         if t == 0:
             iota(A("klo"), [[16, 16]], 16 - C, 0)
             iota(A("cw0"), [[16, 16]], 2 * C, 0, False)
             for b in range(3):
                 unit(b)
-        tt(A("sm", 0, 64), A("p1", 0, 64), A("maskd", 0, 64), ALU.mult)
-        tt(A("sm", 64, C), A("p1", 64, C), A("maskd", 64, C), ALU.mult)
-        tt(A("sm", C, 2 * C), A("p0", 0, C), A("maskd", 0, C), ALU.mult)
-        scan(A("sc", 0, 64), A("c0", 0, 64), A("sm", 0, 64), 0.0, ALU.mult, ALU.add)
-        scan(A("sc", 64, C), A("c0", 64, C), A("sm", 64, C), 0.0, ALU.mult, ALU.add)
-        scan(A("sc", C, 2 * C), A("c0", 0, C), A("sm", C, 2 * C), 0.0, ALU.mult, ALU.add)
-        tt(A("eqf", 0, C), A("p1", 0, C), A("sc", 0, C), ALU.is_equal)
-        tt(A("eqf", C, 2 * C), A("p0", 0, C), A("sc", C, 2 * C), ALU.is_equal)
+            mask(1, 0)
+        hold(0, 0)
+        if t:
+            mask(1, 0)
+        equal(0, 0)
+        hold(1, 0)
+        mask(0, 1)
+        mask(1, 1)
+        equal(1, 0)
+        hold(0, 1)
+        hold(1, 1)
 
-        def compare(flags, bank, base, c):
-            s = A("sc", base + 16 * c + 15, base + 16 * c + 16)
+        def compare(c):
+            s = A("sc", C + 16 * c + 15, C + 16 * c + 16)
             e = 16 * c + 16
-            ts(A(flags, C * c, C * c + e), A(bank, 0, e), s, ALU.is_ge)
+            ts(A("fa", C * c, C * c + e), A("p2", 0, e), s, ALU.is_ge)
             if e < C:
-                ts(A(flags, C * c + e, C * c + C), A(bank, e, C), s, ALU.is_gt)
+                ts(A("fa", C * c + e, C * c + C), A("p2", e, C), s, ALU.is_gt)
 
         def total(out, flags, c, init):
-            scan(A(out, 128 * c, 128 * c + 128), A(flags, C * c, C * c + 128), A(flags, C * c + 128, C * c + C), init, ALU.add, ALU.add)
+            scan(A(out, H * c, H * c + H), A(flags, C * c, C * c + H), A(flags, C * c + H, C * c + C), init, ALU.add, ALU.add)
 
-        for c in range(OWN_S):
-            act(A("sg", C * c, C * c + C), A("p2", 0, C), ACT.Sign, bias=A("sc", 16 * c + 15, 16 * c + 16), scale=-1.0)
-        for c in range(OWN_S):
-            e = 16 * c + 16
-            act(A("sg", C * c, C * c + e), A("sg", C * c, C * c + e), ACT.Relu, accum=A("accl", c, c + 1))
-            if e < C:
-                act(A("sg", C * c + e, C * c + C), A("sg", C * c + e, C * c + C), ACT.Relu, scale=-1.0, accum=A("accg", c, c + 1))
+        for k in range(2):
+            for h in range(2):
+                for c in range(8 * k, 8 * k + 8):
+                    act(A("sg", C * c + H * h, C * c + H * h + H), A("p%d" % (1, 6)[h], 0, H), ACT.Sign,
+                        bias=A("sc", 16 * c + 15, 16 * c + 16), scale=-1.0)
+            for c in range(8 * k, 8 * k + 8):
+                e = 16 * c + 16
+                act(A("sg", C * c, C * c + e), A("sg", C * c, C * c + e), ACT.Relu, accum=A("accl", c, c + 1))
+                if e < C:
+                    act(A("sg", C * c + e, C * c + C), A("sg", C * c + e, C * c + C), ACT.Relu, scale=-1.0, accum=A("accg", c, c + 1))
 
         for c in range(16):
-            compare("fa", "p0", C, c)
+            compare(c)
+            if c == 0:
+                equal(0, 1)
+                equal(1, 1)
             if c == 1:
                 scan(A("eqs"), A("ceq"), A("eqf"), 0.0, ALU.mult, ALU.subtract)
         for c in range(16):
             total("sa", "fa", c, A("eqs", C + 16 * c + 15, C + 16 * c + 16))
+        e = 16 - CROSS_S
         if t == 0:
-            if OWN_S < 16:
-                memset(A("klo", OWN_S, 16), float(-C))
-            copy(A("khi", CROSS_S, 16), A("klo", CROSS_S, 16))
-            ts(A("khi", 0, CROSS_S), A("klo", 0, CROSS_S), float(C), ALU.add)
-        else:
-            tt(A("ke"), A("eqs", 15, C, 16), A("khi" if hi else "klo"), ALU.add)
-        ts(ra_own, A("sa", 127, 2048, 128), float(oo), ALU.add)
+            copy(A("khi", 0, e), A("klo", 0, e))
+            ts(A("khi", e, 16), A("klo", e, 16), float(C), ALU.add)
+        tt(A("dd", 0, 8), A("accg", 0, 8), A("accl", 0, 8), ALU.subtract)
+        tt(A("ke"), A("eqs", 15, C, 16), A("khi" if hi else "klo"), ALU.add)
+        ts(ra_own, A("sa", H - 1, 16 * H, H), float(oo), ALU.add)
         send(t, hi, [3])
         if t == 0:
             unit(3)
-            iota(A("nodet"), [[0, 2], [1, 128], [0, 2]], 0, 0)
-            tt(A("ke"), A("eqs", 15, C, 16), A("khi" if hi else "klo"), ALU.add)
-        for c in range(OWN_S, 16):
-            compare("fo", "p1", 0, c)
+
         arrive(t, hi, [0, 1])
         arrive(t, hi, [2])
         mm(3, "upq", "ups", 128, tq, tsc, C, C)
-        mm(4, "upq", "ups", 128, tq, tsc, C, C)
-        cross = ALU.is_ge if hi else ALU.is_gt
-
-        for c in range(CROSS_S):
-            act(A("sgx", C * c, C * c + C), A("p4", 0, C), ACT.Sign, bias=A("sc", 16 * c + 15, 16 * c + 16), scale=-1.0)
-        for c in range(CROSS_S):
+        mm(7, "upq", "ups", 128, tq, tsc, C, C)
+        for c in range(e, 16):
+            act(A("sgx", C * c, C * c + C), A("p7", 0, C), ACT.Sign, bias=A("sc", 16 * c + 15, 16 * c + 16), scale=-1.0)
+        for c in range(e, 16):
             act(A("sgx", C * c, C * c + C), A("sgx", C * c, C * c + C), ACT.Relu, scale=1.0 if hi else -1.0, accum=A("accx", c, c + 1))
-        for c in range(OWN_S, 16):
-            total("so", "fo", c, A("ke", c, c + 1))
+
+        if t == 0:
+            for k in range(4):
+                act(A("cx", 16 << k, 32 << k), A("cx", 0, 16 << k), ACT.Copy)
 
         def against(c):
-            ts(A("fb", C * c, C * c + C), A("p3", 0, C), A("sc", 16 * c + 15, 16 * c + 16), cross)
+            ts(A("fb", C * c, C * c + C), A("p3", 0, C), A("sc", 16 * c + 15, 16 * c + 16), ALU.is_ge if hi else ALU.is_gt)
 
         def place(c):
-            total("sx", "fb", c, A("own", c, c + 1) if c < OWN_S else A("so", 128 * c + 127, 128 * c + 128))
+            total("sx", "fb", c, A("own", c, c + 1))
 
-        for c in range(8, 16):
+        tt(A("own", 0, 8), A("dd", 0, 8), A("ke", 0, 8), ALU.add)
+        for c in range(9):
             against(c)
-        tt(A("dd", 0, OWN_S), A("accg", 0, OWN_S), A("accl", 0, OWN_S), ALU.subtract)
-        against(7)
-        tt(A("own", 0, OWN_S), A("dd", 0, OWN_S), A("ke", 0, OWN_S), ALU.add)
-        against(6)
-        for c in range(8, 16):
+        for c in range(8):
             place(c)
-        against(5)
-        ts(A(lb, 16 * hi + 8, 16 * hi + 16), A("sx", 128 * 8 + 127, 2048, 128), float(C), ALU.add)
+        against(9)
+        ts(A(lb, 16 * hi, 16 * hi + 8), A("sx", H - 1, 8 * H, H), float(C), ALU.add)
         send(t, hi, [4])
-        for c in range(CROSS_S, 5):
+        tt(A("dd", 8, 16), A("accg", 8, 16), A("accl", 8, 16), ALU.subtract)
+        against(10)
+        tt(A("own", 8, 16), A("dd", 8, 16), A("ke", 8, 16), ALU.add)
+        for c in range(11, e):
             against(c)
-        for c in range(7, CROSS_S - 1, -1):
+        for c in range(8, e - 2):
             place(c)
-            if c == CROSS_S + 1:
-                tt(A("rbm", 0, CROSS_S), A("own", 0, CROSS_S), A("accx", 0, CROSS_S), ALU.subtract if hi else ALU.add)
-        ts(A(lb, 16 * hi, 16 * hi + CROSS_S), A("rbm", 0, CROSS_S), float(C), ALU.add)
-        ts(A(lb, 16 * hi + CROSS_S, 16 * hi + 8), A("sx", 128 * CROSS_S + 127, 1024, 128), float(C), ALU.add)
+        tt(A("rbm", e, 16), A("own", e, 16), A("accx", e, 16), ALU.subtract if hi else ALU.add)
+        for c in range(e - 2, e):
+            place(c)
+        ts(A(lb, 16 * hi + e, 16 * hi + 16), A("rbm", e, 16), float(C), ALU.add)
+        ts(A(lb, 16 * hi + 8, 16 * hi + e), A("sx", H * 8 + H - 1, H * e, H), float(C), ALU.add)
         send(t, hi, [5])
-
-        scatter(A("inva", 0, oo + C), ra_own, A("iotaj", oo, oo + C))
         if t == 0:
             quant(A("eq4"), A("es"), A("eb"))
-        banks = [5, 6, 7, 0]
+
+        banks, banks2 = [4, 0, 1, 6], [5, 2, 3, 7]
+
+        def mates(inv, o, ra):
+            copy(A("invs", o, o + C, 2), A(inv, o + 1, o + C, 2))
+            copy(A("invs", o + 1, o + C, 2), A(inv, o, o + C, 2))
+            act(A("arep", o, o + C), G(A("invs", 0, o + C), ra), ACT.Copy)
+
+        def halved(b):
+            act(A("dpp", C * b, C * b + C), A("p%d" % banks[b], C, 2 * C), ACT.Copy, scale=0.5)
+
+        def picked(b):
+            act(A("g1", C * b, C * b + C), G(A("dpp", C * b, C * b + C), A("inl")), ACT.Copy)
+
+        def mean(b):
+            scan(A("bt", b, 4 * C, 4), A("alt"), A("g1", C * b, C * b + C), 0.0, ALU.mult, ALU.add)
+
+        def unpacked(b, own):
+            if own:
+                act(A("dp", 384 * b, 384 * b + C), A("p%d" % banks[b], 0, C), ACT.Copy)
+            else:
+                act(A("dp", 384 * b + C, 384 * b + 384), A("p%d" % banks2[b], 1, C, 2), ACT.Copy)
+
+        def mate_list(o, step):
+            if step == 0:
+                wrap(("xs3", o), C, A("arep", o, o + C))
+            else:
+                unwrap(A("awl", o // 16, o // 16 + 16), ("xs3", o), C, C - o)
+
         for b in range(4):
             mm(banks[b], "eq4", "es", 128 * b, tq, tsc, 0, 2 * C)
-        for b in range(4):
-            act(A("dpp", C * b, C * b + C), A("p%d" % banks[b], C, 2 * C), ACT.Copy, scale=0.5)
+        for b in range(2):
+            halved(b)
+            unpacked(b, True)
         arrive(t, hi, [3])
-        scatter(A("inva", 0, po + C), ra_par, A("iotaj", po, po + C))
-        act(A("dp", 0, C), A("p%d" % banks[0], 0, C), ACT.Copy)
+        scatter(A("inva", 0, oo + C), ra_own, A("iotaj", oo, oo + C))
+        scatter(A("inw", 0, po + C), A(msg, 16 * (1 - hi), 16 * (1 - hi) + 8), A("iotaj", po, po + H))
+        mates("inva", oo, ra_own)
+        scatter(A("inw", 0, po + C), A(msg, 16 * (1 - hi) + 8, 16 * (1 - hi) + 16), A("iotaj", po + H, po + C))
         if t == 0:
             ts(A("cw"), A("cw0"), A("rf", 0, 1), ALU.add)
-            ts(A("cf"), A("cw0"), A("rf", 0, 1), ALU.add, float(-2 * C), ALU.add)
-        wrap(("xs", 0), 128, A("inva", po, po + C, 2))
-        wrap(("xs", 128), 128, A("inva", po + 1, po + C, 2))
-        copy(A("invs", 0, 2 * C, 2), A("inva", 1, 2 * C, 2))
-        copy(A("invs", 1, 2 * C, 2), A("inva", 0, 2 * C, 2))
-        unwrap(A("evl"), ("xs", 0), C, C - po)
-        copy(A("arep", oo, oo + C), G(A("invs"), ra_own))
-        for b in range(4):
-            act(A("g1", 128 * b, 128 * b + 128), G(A("dpp", C * b, C * b + C), A("evl", 0, 8)), ACT.Copy)
-            if b == 1:
-                act(A("arep", po, po + C), G(A("invs"), ra_par), ACT.Copy)
-        tt(A("bt", 0, 512, 4), G(A("dpp", 0, C), A("evl", 8, 16)), A("g1", 0, 128), ALU.add)
-        scatter(A("mm"), A(lb, 16 * hi, 16 * hi + 16), A("arep", oo, oo + C))
+            copy(A("cx2", 0, C, 2), A("cx", 0, H))
         if t == 1:
             quant(A("vq"), A("vs"), A("vb"))
-        for b in range(1, 4):
-            tt(A("bt", b, 512, 4), G(A("dpp", C * b, C * b + C), A("evl", 8, 16)), A("g1", 128 * b, 128 * b + 128), ALU.add)
+        mates("inw", po, ra_par)
+        halved(2)
+        halved(3)
+        wrap(("xs4", 0), C, A("inw", po, po + C))
+        scatter(A("mm"), A(lb, 16 * hi, 16 * hi + 16), A("arep", oo, oo + C))
+        unwrap(A("inl"), ("xs4", 0), C, C - po)
+        for b in range(3):
+            picked(b)
         arrive(t, hi, [4])
-        scatter(A("mm"), A(lb, 16 * (1 - hi) + 8, 16 * (1 - hi) + 16), A("arep", po + 128, po + C))
-        quant(A("bq"), A("bs"), A("bt"))
-        for b in range(4):
-            mm(1 + b, "eq4", "es", 128 * b, "bq", "bs", 0, 128)
-        for b in range(1, 4):
-            act(A("dp", 384 * b, 384 * b + C), A("p%d" % banks[b], 0, C), ACT.Copy)
+        scatter(A("mm"), A(lb, 16 * (1 - hi), 16 * (1 - hi) + 8), A("arep", po, po + H))
+        mate_list(oo, 0)
 
         arrive(t, hi, [5])
-        scatter(A("mm"), A(lb, 16 * (1 - hi), 16 * (1 - hi) + 8), A("arep", po, po + 128))
+        scatter(A("mm"), A(lb, 16 * (1 - hi) + 8, 16 * (1 - hi) + 16), A("arep", po + H, po + C))
+        mate_list(oo, 1)
         copy(A("ms", 0, 512, 2), A("mm", 1, 512, 2))
         copy(A("ms", 1, 512, 2), A("mm", 0, 512, 2))
-        act(A("pa", C, 2 * C), G(A("ms"), A(lb, 16, 32)), ACT.Copy)
-        copy(A("pa", 0, C), G(A("ms"), A(lb, 0, 16)))
-        P, low = ["pa", "pb"], ["lowa", "lowb"]
+        mate_list(po, 0)
+        P, low, twin = ["pa", "pb"], ["lowa", "lowb"], ["lowc", "lowd"]
+        side = (po, oo)
 
-        def listed(k, h, step):
-            tmp = ("xs" if k % 2 else "xs2", C * h)
-            if step == 0:
-                wrap(tmp, C, A(P[k % 2], C * h, C * h + C))
+        def square(k, h):
+            o = side[h]
+            was = G(A(P[1 - k % 2]), A("ll", 32 * k + o // 16 - 32, 32 * k + o // 16 - 16)) if k else G(A("ms"), A(lb, o // 16, o // 16 + 16))
+            act(A(P[k % 2], o, o + C), was, ACT.Copy)
+
+        def held(k, h):
+            wrap(("xs" if k % 2 else "xs2", side[h]), C, A(P[k % 2], side[h], side[h] + C))
+
+        def listed(k, h):
+            unwrap(A("ll", 32 * k + side[h] // 16, 32 * k + side[h] // 16 + 16), ("xs" if k % 2 else "xs2", side[h]), C, C)
+
+        def least(k, h, a=0, b=C):
+            a, b = side[h] + a, side[h] + b
+            if k:
+                tt(A(low[k % 2], a, b), G(A(low[1 - k % 2]), A("ll", 32 * k + a // 16, 32 * k + b // 16)), A(twin[1 - k % 2], a, b), ALU.min)
             else:
-                unwrap(A("ll", 32 * k + 16 * h, 32 * k + 16 * h + 16), tmp, C, C)
+                scan(A(low[0], a, b), A("iotaj", a, b), A(P[0], a, b), -1024.0, ALU.max, ALU.min)
 
-        def least(k, a, b):
-            win, other = (A("iotaj"), "iotak") if k == 0 else (A(low[k % 2]), "lowc")
-            tt(A(low[(k + 1) % 2], a, b), G(win, A("ll", 32 * k + a // 16, 32 * k + b // 16)), A(other, a, b), ALU.min)
+        def again(k, h, a=0, b=C, vector=False):
+            a, b = side[h] + a, side[h] + b
+            if a < b and vector:
+                copy(A(twin[k % 2], a, b), A(low[k % 2], a, b))
+            elif a < b:
+                act(A(twin[k % 2], a, b), A(low[k % 2], a, b), ACT.Copy)
 
-        def again(k, a, b, to="lowc"):
-            act(A(to, a, b), A(low[(k + 1) % 2], a, b), ACT.Copy)
-
-        listed(0, 0, 0)
-        listed(0, 1, 0)
-        listed(0, 0, 1)
-        listed(0, 1, 1)
-        for k in range(DOUBLINGS - 1):
-            for h in range(2):
-                act(A(P[(k + 1) % 2], C * h, C * h + C), G(A(P[k % 2]), A("ll", 32 * k + 16 * h, 32 * k + 16 * h + 16)), ACT.Copy)
-            if k > 0:
-                again(k - 1, 384, 512)
-            least(k, 0, C)
-            again(k, 0, C)
-            listed(k + 1, 0, 0)
-            least(k, C, 384)
-            listed(k + 1, 0, 1)
-            listed(k + 1, 1, 0)
-            least(k, 384, 512)
-            again(k, C, 384)
-            listed(k + 1, 1, 1)
-            if k < 4:
-                wrap(("xs3", 128 * k), 128, A("arep", 128 * k, 128 * k + 128))
-            elif k == 4:
-                unwrap(A("awl"), ("xs3", 0), 512, C)
+        copy(A(P[0], po, po + C), G(A("ms"), A(lb, po // 16, po // 16 + 16)))
+        square(0, 1)
+        picked(3)
+        mate_list(po, 1)
+        held(0, 0)
+        least(0, 0)
+        listed(0, 0)
+        held(0, 1)
+        square(1, 0)
+        least(0, 1)
+        listed(0, 1)
+        square(1, 1)
+        again(0, 0, vector=True)
+        again(0, 1, vector=True)
+        mean(0)
+        held(1, 0)
+        mean(1)
+        listed(1, 0)
+        held(1, 1)
+        mean(2)
+        listed(1, 1)
+        for k in range(1, DOUBLINGS - 1):
+            square(k + 1, 0)
+            if k > 1:
+                again(k - 1, 1, 0, H)
+            square(k + 1, 1)
+            least(k, 0)
+            again(k, 0)
+            held(k + 1, 0)
+            least(k, 1, 0, H)
+            listed(k + 1, 0)
+            least(k, 1, H, C)
+            held(k + 1, 1)
+            again(k, 1, H, C, True)
+            listed(k + 1, 1)
         k = DOUBLINGS - 1
-        again(k - 1, 384, 512)
-        for h in (1 - hi, hi):
-            least(k, C * h, C * h + C)
-            again(k, C * h, C * h + C, "pa")
-        act(A("nodep"), G(A("nodet"), ra_par), ACT.Copy)
-        for b in range(4):
-            act(A("dp", 384 * b + C, 384 * b + 384), A("p%d" % (1 + b), 0, 128), ACT.Copy)
+        again(k - 1, 1, 0, H)
+        least(k, 0)
+        unpacked(2, True)
+        unpacked(3, True)
+        again(k, 0)
+        least(k, 1)
+        again(k, 1)
+        mean(3)
 
-        lw = low[DOUBLINGS % 2]
+        lw, tw = low[1 - DOUBLINGS % 2], twin[1 - DOUBLINGS % 2]
 
         def fl(h, shift):
             return A("fl", 16 + 272 * h - shift, 272 + 272 * h - shift)
 
-        for h in (1 - hi, hi):
-            tt(fl(h, 0), G(A(lw, 0, C * h + C), A("awl", 16 * h, 16 * h + 16)), A("pa", C * h, C * h + C), ALU.is_gt)
-        scan(A("vv", po, po + C), fl(1 - hi, 0), fl(1 - hi, 1), 0.0, ALU.add, ALU.add)
-        wrap(("xs2", 0), C, fl(1 - hi, 0))
-        scan(A("vv", oo, oo + C), fl(hi, 0), fl(hi, 1), 0.0, ALU.add, ALU.add)
-        wrap(("xs", 0), C, A("vv", po, po + C))
-        ts(A("tf"), A("xs2", 15, C, 16), A("scl", 0, 1), ALU.mult, 1024.0, ALU.mult)
-        wrap(("xs", C), C, A("vv", oo, oo + C))
-        unwrap(A("wf"), ("xs", 0), C, 513)
-        tt(A("tg"), A("tf"), A("cf"), ALU.add)
-        unwrap(A("lu", 16, 32), ("xs", C), C, 513)
-        tt(A("lf"), A("tg"), A("wf"), ALU.min)
-        if last:
-            unwrap(A("wi", 16, 32), ("xs", C), C, 1)
-        copy(A("lu", 0, 16), A("lf"))
-        if last:
-            ts(A("nf", 16, 32), A("wi", 16, 32), 1, ALU.bitwise_and)
-            ts(A("hh", 16, 32), A("wi", 16, 32), 1, ALU.arith_shift_right)
-        scatter(A("wn"), A("lu", 0, 16), A("nodep"))
-        if last:
-            tt(A("tc", 16, 32), A("nf", 16, 32), A("cw"), ALU.mult)
-        for h in range(2):
-            tt(A("yv", 128 * h, 128 * h + 128), G(A("wn"), A("lu", 16 + 8 * h, 24 + 8 * h)), A("iotaj", 128 * h, 128 * h + 128), ALU.max)
-        for h in range(2):
-            wrap(("xs2", 128 * h), 128, A("yv", 128 * h, 128 * h + 128))
-        if last:
-            tt(A("lm", 16, 32), A("tc", 16, 32), A("hh", 16, 32), ALU.max)
-        for h in range(2):
-            unwrap(A("yl", 8 * h, 8 * h + 8), ("xs2", 128 * h), 128, C)
-        if last:
-            copy(A("ol16"), A("lm", 16, 32))
+        def flags(h):
+            tt(fl(h, 0), G(A(lw, C * h, C * h + C), A("awl", 16 * h, 16 * h + 16)), A(tw, C * h, C * h + C), ALU.is_gt)
 
-        H = C // HALVES
-        for h in range(HALVES):
-            for b in range(4):
-                win = G(A("dp", 384 * b, 384 * b + 384), A("yl", H // 16 * h, H // 16 * (h + 1)))
-                if b % 2:
-                    act(A("yt", 4 * H * h + b, 4 * H * (h + 1), 4), win, ACT.Copy)
-                else:
-                    copy(A("yt", 4 * H * h + b, 4 * H * (h + 1), 4), win)
+        flags(1 - hi)
+        act(A("fa1"), fl(1 - hi, 0), ACT.Copy, scale=129.0)
+        flags(hi)
+        ts(A("fb1", 16, 272), fl(1 - hi, 0), -128.0, ALU.mult)
+        quant(A("bq"), A("bs"), A("bt"))
+        for b in range(4):
+            mm(banks2[b], "eq4", "es", 128 * b, "bq", "bs", 0, C)
+            unpacked(b, False)
+        scan(A("sp"), A("fa1"), A("fb1", 15, 271), 0.0, ALU.add, ALU.add)
+        scan(A("vv"), fl(hi, 0), fl(hi, 1), 0.0, ALU.add, ALU.add)
+        copy(A("ge"), G(A("sp"), A("inl")))
+        wrap(("xs6", 0), H, A("vv", 0, H))
+        scan(A("xs5"), A("cx2"), A("ge"), 0.0, ALU.mult, ALU.max)
+        wrap(("xs6", H), H, A("vv", H, C))
+        ts(A("kl"), A("xs5", 31, C, 32), A("scl2", 0, 1), ALU.mult, -257.0, ALU.add)
+        unwrap(A("lu", 0, 8), ("xs6", 0), H, 0)
+        scatter(A("wn"), A("kl"), A("iotaj", C, C + H))
+        unwrap(A("lu", 8, 16), ("xs6", H), H, 0)
+        for h in range(2):
+            tt(A("yv", H * h, H * h + H), G(A("wn"), A("lu", 8 * h, 8 + 8 * h)), A("iotaj", H * h, H * h + H), ALU.max)
+        for h in range(2):
+            wrap(("xs7", H * h), H, A("yv", H * h, H * h + H))
+        for h in range(2):
+            unwrap(A("yl", 8 * h, 8 * h + 8), ("xs7", H * h), H, C)
+
+        nq, nsc = "tq%d" % (t + 1), "ts%d" % (t + 1)
+
+        def part(h, b, vector):
+            win = G(A("dp", 384 * b, 384 * b + 384), A("yl", 8 * h, 8 * h + 8))
+            if vector:
+                copy(A("yt", 4 * H * h + b, 4 * H * (h + 1), 4), win)
+            else:
+                act(A("yt", 4 * H * h + b, 4 * H * (h + 1), 4), win, ACT.Copy)
+
+        def packed(h):
             quant(A("zq", H * h, H * h + H), A("zs", H * h, H * h + H), A("yt", 4 * H * h, 4 * H * (h + 1)))
-        for h in range(HALVES):
-            for b in (0, 1, 4, 2, 5, 3, 6, 7):
-                mm(b, "wq" if b < 4 else "eq4", "wsc" if b < 4 else "es", 128 * (b % 4), "zq", "zs", H * h, H)
-            for b in range(4):
+
+        def products(h, bs):
+            for b in bs:
+                mm(b, "wq", "wsc", 128 * b, "zq", "zs", H * h, H)
+            for b in bs:
+                mm(4 + b, "eq4", "es", 128 * b, "zq", "zs", H * h, H)
+
+        def relu(h, b, vector=False):
+            if vector:
+                ts(A("rr", C * b + H * h, C * b + H * h + H), A("p%d" % b, 0, H), 0.0, ALU.max, 0.03125, ALU.mult)
+            else:
                 act(A("rr", C * b + H * h, C * b + H * h + H), A("p%d" % b, 0, H), ACT.Relu, scale=0.03125)
-                tt(A("xn", 4 * H * h + b, 4 * H * (h + 1), 4), A("p%d" % (4 + b), 0, H), A("rr", C * b + H * h, C * b + H * h + H), ALU.add)
 
-    tq, tsc = "tq%d" % ROUNDS, "ts%d" % ROUNDS
+        def new(h, b):
+            tt(A("xn", 4 * H * h + b, 4 * H * (h + 1), 4), A("p%d" % (4 + b), 0, H), A("rr", C * b + H * h, C * b + H * h + H), ALU.add)
 
-    def scales(queue, k):
-        dma(queue, T.osc[4 * k:4 * k + 4, :], T[tsc][32 * k:32 * k + 4, 0:C], [A(tsc)], [])
+        def state(h):
+            quant(A(nq, H * h, H * h + H), A(nsc, H * h, H * h + H), A("xn", 4 * H * h, 4 * H * (h + 1)))
 
-    quant(A(tq), A(tsc), A("xn"))
-    mm(0, "vq", "vs", 0, tq, tsc, 0, C)
-    dma("sync", T.oc[:, :], T[tq][:, 0:C].bitcast(dt.uint8), [A(tq)], [])
-    scatter(A("wo"), A("ol16"), A("iotaj", C, 2 * C))
-    scales("sync", 0)
-    scales("scalar", 1)
-    scales("sync", 2)
-    act(A("yo"), A("p0", 0, C), ACT.Copy)
-    dma("scalar", T.y[:, :], T.yo[:], [A("yo")], [])
-    scales("scalar", 3)
-    dma("sync", T.ol[:, :], T.wo[0:128:16, 1:129], [A("wo")], [])
+        reds = []
+        if last:
+            reds = [lambda: unwrap(A("wi"), ("xs6", 0), C, 1), lambda: ts(A("nf"), A("wi"), 1, ALU.bitwise_and),
+                    lambda: ts(A("hh"), A("wi"), 1, ALU.arith_shift_right), lambda: tt(A("tc"), A("nf"), A("cw"), ALU.mult),
+                    lambda: tt(A("lm"), A("tc"), A("hh"), ALU.max), lambda: copy(A("ol16"), A("lm"))]
+
+        def red(n=1):
+            for k in range(n):
+                if reds:
+                    reds.pop(0)()
+
+        for b in range(3):
+            red()
+            part(0, b, True)
+        part(0, 3, False)
+        red()
+        part(1, 0, True)
+        red()
+        packed(0)
+        products(0, range(4))
+        part(1, 2, False)
+        part(1, 3, False)
+        red()
+        part(1, 1, True)
+        if last:
+            scatter(A("wo"), A("ol16", 0, 8), A("iotaj", C, C + H))
+        packed(1)
+        for b in range(4):
+            relu(0, b, b < 2)
+        for b in range(4):
+            new(0, b)
+        products(1, (0, 1))
+        products(1, (2, 3))
+        state(0)
+        if last:
+            results(0)
+        else:
+            send(t + 1, 1 if rank & STEP[t + 1] else 0, [0])
+        for b in range(4):
+            relu(1, b)
+            new(1, b)
+            if b == 1 and not last:
+                scores(t + 1, 0)
+        if last:
+            scatter(A("wo"), A("ol16", 8, 16), A("iotaj", C + H, 2 * C))
+            dma("sync", T.ol[:, :], T.wo[0:128:16, 1:129], [A("wo")], [])
+        else:
+            mask(0, 0)
+        state(1)
+
+    results(1)
+    for k in range(4):
+        dma("sync", T.osc[4 * k:4 * k + 4, :], T["ts%d" % ROUNDS][32 * k:32 * k + 4, 0:C], [A("ts%d" % ROUNDS)], [])
     emit(g, T, ops, left[0])

@@ -8,22 +8,22 @@ H = C // 2
 ROUNDS = 3
 STEP = [1, 2, 4]
 DOUBLINGS = 8
-CROSS_S = 3
-SPLIT = 128
+CROSS_S = 4
+FIRST = 8
 BIG = 2.0 ** 40
 Q4, U8, BF, F32, I32, U16 = "float8_e4m3fn_x4", "uint8", "bfloat16", "float32", "int32", "uint16"
 
 SCRATCH = {}
 for _d, _l in [
     (BF, "x0 1024 xn 1024 ub 512 vb 512 ones 512 eb 2048 t16 512 maskd 128 ceq 512 c0 128 cx 256 ctmp 16 iotaj 512 "
-         "cx2 256 wn 272 eqf 512 eqs 512 fa 4096 fb 4096 sa 2048 sx 2048 sg 4096 sgx 4096 inva 512 inw 512 invs 512 "
-         "arep 512 xs 512 xs2 512 xs3 512 xs4 256 xs5 256 xs6 256 xs7 256 mm 512 ms 512 pa 512 pb 512 lowa 512 lowb 512 lowc 512 lowd 512 "
-         "fl 544 vv 256 fa1 256 fb1 272 sp 256 ge 256 yv 256 dp 1536 dpp 1024 g1 1024 bt 1024 alt 256 yt 1024"),
+         "cx2 256 wn 272 eqf 512 eqs 512 fa 4096 fb 4096 sa 2048 sx 2048 sg 4096 sgx 4096 inva 256 inw 256 invs 512 "
+         "arep 512 xs 512 xs2 512 xs3 256 xs4 256 xs5 256 xs6 256 xs7 256 mm 512 ms 512 pa 512 pb 512 lowa 512 lowb 512 lowc 512 lowd 512 "
+         "fl 544 vv 256 fa1 256 fb1 272 sp 256 ge 256 yv 256 yw 128 dp 1536 dpp 1024 g1 1024 bt 1024 alt 256 yt 1024"),
     (Q4, "uq 128 upq 256 vq 128 wq 512 eq4 512 bq 256 zq 256 tq0 512 tq1 512 tq2 512 tq3 256"),
     (U8, "us 128 ups 256 vs 128 wsc 512 es 512 bs 256 zs 256 ts0 512 ts1 512 ts2 512 ts3 256"),
     (I32, "pcol 8 rcol 8 offi 16 cw0 16 cw 16 wi 16 hh 16 nf 16 tc 16 lm 16"),
-    (F32, "rf 8 rf1 8 scl 8 scl2 8 klo 16 khi 16 wo 768 sm 512 sc 512 accl 16 accg 16 accx 16 ke 16 dd 16 own 16 rbm 16 rr 1024 yo 256"),
-    (U16, "offu 16 inl 16 awl 32 ll 256 lu 16 kl 8 yl 16 ol16 16 msg0 32 msg1 32 msg2 32 lb0 32 lb1 32 lb2 32"),
+    (F32, "rf 8 rf1 8 scl 8 scl2 8 klo 16 khi 16 wo 768 sm 512 sc 512 accl 16 accg 16 accx 16 ke 16 dd 16 own 16 rr 1024 yo 256"),
+    (U16, "offu 16 inl 16 ll 256 lu 16 kl 8 yl 16 ol16 16 ra 96 rb 96 am 96"),
 ]:
     _w = _l.split()
     for _i in range(0, len(_w), 2):
@@ -31,9 +31,9 @@ for _d, _l in [
 for _b in range(8):
     SCRATCH["p%d" % _b] = ("psum", [128, 512], F32)
 
-SEMAPHORES = ["s_vector", "s_scalar", "s_tensor", "s_pool", "left"] + ["dma%d" % _k for _k in range(16)]
+SEMAPHORES = ["s_vector", "s_scalar", "s_tensor", "s_pool", "left"] + ["dma%d" % _k for _k in range(20)]
 for _t in range(ROUNDS):
-    SEMAPHORES += ["at%d" % _t, "as%d" % _t, "am%d" % _t, "ar%d" % _t, "aq%d" % _t]
+    SEMAPHORES += [_n + str(_t) for _n in ("codes0", "codes1", "scales0", "scales1", "ra", "rb0", "rb1", "am")]
 
 
 def _mask(engines):
@@ -49,19 +49,23 @@ def relays(T, topo, src, dst):
     return r[:4]
 
 
-def pieces(t, hi):
-    o = 16 * hi
-    out = [(1 + k, "tq%d" % t, (128 * k, 128 * k + 128), (C + 128 * k, C + 128 * k + 128), "at%d" % t, True) for k in range(2)]
-    out.append((3, "ts%d" % t, (0, C), (C, 2 * C), "as%d" % t, False))
-    out.append((0, "msg%d" % t, (o, o + 16), (o, o + 16), "am%d" % t, False))
-    out.append((1, "lb%d" % t, (o, o + 8), (o, o + 8), "aq%d" % t, False))
-    out.append((0, "lb%d" % t, (o + 8, o + 16), (o + 8, o + 16), "ar%d" % t, False))
+def messages(t, hi):
+    out = {}
+    for h in range(2):
+        cuts = [H * h + H // 2 * k for k in range(2)]
+        out["codes%d" % h] = [(h + 2 * k, "tq%d" % t, (a, a + H // 2), (C + a, C + a + H // 2)) for k, a in enumerate(cuts)]
+        out["scales%d" % h] = [(1 + h, "ts%d" % t, (H * h, H * h + H), (C + H * h, C + H * h + H))]
+    o = 32 * t + 16 * hi
+    out["ra"] = [(0, "ra", (o, o + 16), (o, o + 16))]
+    out["rb0"] = [(1, "rb", (o, o + FIRST), (o, o + FIRST))]
+    out["rb1"] = [(0, "rb", (o + FIRST, o + 16), (o + FIRST, o + 16))]
+    out["am"] = [(1, "am", (o, o + 16), (o, o + 16))]
     return out
 
 
-def view(T, name, cols, codes):
+def view(T, name, cols):
     ap = T[name][:, cols[0]:cols[1]]
-    return ap.bitcast(dt.uint8) if codes else ap
+    return ap.bitcast(dt.uint8) if SCRATCH[name][2] == Q4 else ap
 
 
 def relay_program(g, core, T, topo):
@@ -71,13 +75,15 @@ def relay_program(g, core, T, topo):
         for t in range(ROUNDS):
             dst = T.cores[r ^ STEP[t]]
             rel = relays(T, topo, src, dst)
-            for k, name, a, b, sem, codes in pieces(t, 1 if r & STEP[t] else 0):
-                if rel[k] != core:
-                    continue
-                g.wait_ge(T.sem[sem], len(topo.engines(src, core)))
-                rid, pid = topo.addr(dst, core)
-                g.remote_dma(view(T, name, b, codes), view(T, name, b, codes), T.sem[sem], T.sem.left, pid, rid, topo.mask(core, dst))
-                left += len(topo.engines(core, dst))
+            for what, ps in messages(t, 1 if r & STEP[t] else 0).items():
+                for k, name, a, b in ps:
+                    if rel[k] != core:
+                        continue
+                    sem = T.sem[what + str(t)]
+                    g.wait_ge(sem, len(topo.engines(src, core)) // len(ps))
+                    rid, pid = topo.addr(dst, core)
+                    g.remote_dma(view(T, name, b), view(T, name, b), sem, T.sem.left, pid, rid, topo.mask(core, dst))
+                    left += len(topo.engines(core, dst))
     if left:
         g.wait_ge(T.sem.left, left)
 
@@ -229,35 +235,35 @@ def rank_program(g, core, T, topo):
         out = A("eb", 512 * b, 512 * b + 512)
         add("pool", lambda q: q.affine_select(out[0], T.ones[:], [[-1, 512]], ALU.is_equal, 0.0, b, 4), [A("ones")], [out])
 
+    def keep(out, in_, n):
+        add("pool", lambda q: q.affine_select(out[0], in_[0], [[0, n]], ALU.is_ge, 0.0, 0, 0), [in_], [out])
+
     def dma(queue, out, in_, r, w):
         add(queue, lambda q: q.dma_start(out, in_), r, w, "dma")
 
-    def send(t, hi, which):
-        dst = T.cores[rank ^ STEP[t]]
-        rel = relays(T, topo, core, dst)
-        ps = [pieces(t, hi)[k] for k in which]
-        if len(ps) > 1:
-            trs = []
-            for i, (k, name, a, b, sem, codes) in enumerate(ps):
-                eng = topo.engines(core, rel[k])
-                n = len(eng) // len(ps)
-                rid, pid = topo.addr(rel[k], core)
-                trs.append(RemoteDMATransfer(dst_ids=[DstId(rid=rid, pnc=pid)], dma_engine_mask=_mask(eng[n * i:n * i + n]),
-                                             remote_sem=T.sem[sem], src=view(T, name, a, codes), dst=view(T, name, b, codes)))
-                left[0] += n
-            add("pool", lambda q: q.remote_dma_fused(trs, local_sem=T.sem.left), [A(p[1], p[2][0], p[2][1]) for p in ps], [], "send")
-        else:
-            k, name, a, b, sem, codes = ps[0]
+    def send(t, what):
+        rel = relays(T, topo, core, T.cores[rank ^ STEP[t]])
+        ps = messages(t, 1 if rank & STEP[t] else 0)[what]
+        trs = []
+        for i, (k, name, a, b) in enumerate(ps):
+            eng = topo.engines(core, rel[k])
+            n = len(eng) // len(ps)
             rid, pid = topo.addr(rel[k], core)
-            left[0] += len(topo.engines(core, rel[k]))
-            add("pool", lambda q: q.remote_dma(view(T, name, b, codes), view(T, name, a, codes), T.sem[sem], T.sem.left, pid, rid,
-                                               topo.mask(core, rel[k])), [A(name, a[0], a[1])], [], "send")
+            trs.append((view(T, name, b), view(T, name, a), pid, rid, _mask(eng[n * i:n * i + n])))
+            left[0] += n
+        sem = T.sem[what + str(t)]
+        if len(ps) > 1:
+            fused = [RemoteDMATransfer(dst_ids=[DstId(rid=rid, pnc=pid)], dma_engine_mask=m, remote_sem=sem, src=a, dst=b)
+                     for b, a, pid, rid, m in trs]
+            add("pool", lambda q: q.remote_dma_fused(fused, local_sem=T.sem.left), [A(p[1], *p[2]) for p in ps], [], "send")
+        else:
+            b, a, pid, rid, m = trs[0]
+            add("pool", lambda q: q.remote_dma(b, a, sem, T.sem.left, pid, rid, m), [A(p[1], *p[2]) for p in ps], [], "send")
 
-    def arrive(t, hi, which):
-        src = T.cores[rank ^ STEP[t]]
-        rel = relays(T, topo, src, core)
-        ps = [pieces(t, 1 - hi)[k] for k in which]
-        ops.append({"q": None, "kind": "arrive", "r": [], "w": [(p[1], p[3][0], p[3][1], 1) for p in ps], "sem": ps[0][4],
+    def arrive(t, what):
+        rel = relays(T, topo, T.cores[rank ^ STEP[t]], core)
+        ps = messages(t, 0 if rank & STEP[t] else 1)[what]
+        ops.append({"q": None, "kind": "arrive", "r": [], "w": [(p[1], p[3][0], p[3][1], 1) for p in ps], "sem": what + str(t),
                     "val": sum(len(topo.engines(rel[p[0]], core)) for p in ps)})
 
     def wrap(tmp, n, src):
@@ -266,22 +272,23 @@ def rank_program(g, core, T, topo):
     def unwrap(out, tmp, n, plus):
         ts(out, A(tmp[0], tmp[1] + 15, tmp[1] + n, 16), A("scl", 0, 1), ALU.mult, float(plus), ALU.add)
 
-    dma("sync", T.x0[:], T.x[:], [], [A("x0")])
-    dma("scalar", T.ub[:], T.u[:], [], [A("ub")])
+    dma("sync", T.ub[:], T.u[:], [], [A("ub")])
+    dma("scalar", T.x0[:, 0:2 * C], T.x[:, 0:2 * C], [], [A("x0", 0, 2 * C)])
+    dma("sync", T.x0[:, 2 * C:4 * C], T.x[:, 2 * C:4 * C], [], [A("x0", 2 * C, 4 * C)])
     dma("sync", T.wq[:].bitcast(dt.uint8), T.wc[:], [A("x0")], [A("wq")])
     dma("sync", T.wsc[:], T.ws[:], [], [A("wsc")])
     dma("sync", T.vb[:], T.v[:], [], [A("vb")])
-    iota(A("pcol", 0, 1), [[0, 1]], 0, 1, False)
     iota(A("offi"), [[8, 2], [16, 8]], 0, 0, False)
+    iota(A("pcol", 0, 1), [[0, 1]], 0, 1, False)
     iota(A("t16"), [[0, 32], [1, 16]], 0, 0)
     iota(A("iotaj"), [[1, 512]], -C, 0)
     memset(A("ones"), 1.0)
-    ts(A("rcol", 0, 1), A("pcol", 0, 1), 15, ALU.bitwise_and)
     copy(A("offu"), A("offi"))
+    ts(A("rcol", 0, 1), A("pcol", 0, 1), 15, ALU.bitwise_and)
     memset(A("accg"), 0.0)
     memset(A("fl"), 0.0)
     copy(A("rf", 0, 1), A("rcol", 0, 1))
-    memset(A("wn"), -1024.0)
+    memset(A("wn"), 1024.0)
     memset(A("fb1", 0, 16), 0.0)
     memset(A("cx2", 1, C, 2), 1.0)
     memset(A("alt", 0, C, 2), 0.0)
@@ -291,15 +298,20 @@ def rank_program(g, core, T, topo):
     ts(A("maskd"), A("t16", 0, H), A("rf", 0, 1), ALU.is_equal)
     ts(A("c0"), A("t16", 0, H), 0.0, ALU.not_equal)
     ts(A("ctmp"), A("t16", 0, 16), A("rf1", 0, 1), ALU.is_equal, BIG, ALU.mult)
-    ts(A("scl2", 0, 1), A("scl", 0, 1), 2.0, ALU.mult)
     quant(A("uq"), A("us"), A("ub"))
-    ts(A("ceq"), A("t16"), A("rf", 0, 1), ALU.not_equal)
+    quant(A("tq0", 0, H), A("ts0", 0, H), A("x0", 0, 4 * H))
     add("vector", lambda q: q.tensor_copy(T.upq[:, 0:256].bitcast(dt.uint32), T.uq[:, 0:128].bitcast(dt.uint32).indirect(T.offu[:, 0:16])),
         [A("uq"), A("offu")], [A("upq")])
     add("scalar", lambda q: q.activation(T.ups[:, 0:256], T.us[:, 0:128].indirect(T.offu[:, 0:16]), ACT.Copy),
         [A("us"), A("offu")], [A("ups")])
-    tt(A("cx", 0, 16), A("ctmp"), A("ceq", 0, 16), ALU.add)
-    quant(A("tq0", 0, C), A("ts0", 0, C), A("x0"))
+
+    def state(t, h):
+        quant(A("tq%d" % t, H * h, H * h + H), A("ts%d" % t, H * h, H * h + H), A("xn" if t else "x0", 4 * H * h, 4 * H * (h + 1)))
+        if t < ROUNDS:
+            send(t, "codes%d" % h)
+            send(t, "scales%d" % h)
+        else:
+            dma("sync", T.oc[:, 4 * H * h:4 * H * (h + 1)], T["tq%d" % t][:, H * h:H * h + H].bitcast(dt.uint8), [A("tq%d" % t, H * h, H * h + H)], [])
 
     def scores(t, h):
         tq, tsc = "tq%d" % t, "ts%d" % t
@@ -321,43 +333,41 @@ def rank_program(g, core, T, topo):
         o = C * k + H * h
         tt(A("eqf", o, o + H), half(k, h), A("sc", o, o + H), ALU.is_equal)
 
-    def results(h):
-        tq, tsc = "tq%d" % ROUNDS, "ts%d" % ROUNDS
-        dma("sync", T.oc[:, 4 * H * h:4 * H * (h + 1)], T[tq][:, H * h:H * h + H].bitcast(dt.uint8), [A(tq, H * h, H * h + H)], [])
-        if h:
-            mm(0, "vq", "vs", 0, tq, tsc, 0, C)
-            act(A("yo"), A("p0", 0, C), ACT.Copy)
-            dma("scalar", T.y[:, :], T.yo[:], [A("yo")], [])
+    def result(h):
+        mm(h, "vq", "vs", 0, "tq%d" % ROUNDS, "ts%d" % ROUNDS, H * h, H)
+        act(A("yo", H * h, H * h + H), A("p%d" % h, 0, H), ACT.Copy)
+        dma("scalar", T.y[:, H * h:H * h + H], T.yo[:, H * h:H * h + H], [A("yo", H * h, H * h + H)], [])
 
-    send(0, rank & STEP[0], [0])
+    send(0, "codes0")
+    send(0, "scales0")
     scores(0, 0)
+    state(0, 1)
+    ts(A("ceq"), A("t16"), A("rf", 0, 1), ALU.not_equal)
+    ts(A("scl2", 0, 1), A("scl", 0, 1), 2.0, ALU.mult)
     mask(0, 0)
     for t in range(ROUNDS):
         hi = 1 if rank & STEP[t] else 0
         last = t == ROUNDS - 1
         oo, po = C * hi, C * (1 - hi)
-        tq, tsc, msg, lb = "tq%d" % t, "ts%d" % t, "msg%d" % t, "lb%d" % t
-        ra_own, ra_par = A(msg, 16 * hi, 16 * hi + 16), A(msg, 16 * (1 - hi), 16 * (1 - hi) + 16)
+        tq, tsc = "tq%d" % t, "ts%d" % t
 
-        send(t, hi, [1])
-        send(t, hi, [2])
+        def L(name, o, a=0, b=16):
+            return A(name, 32 * t + o // 16 + a, 32 * t + o // 16 + b)
+
         scores(t, 1)
         if t == 0:
             iota(A("klo"), [[16, 16]], 16 - C, 0)
             iota(A("cw0"), [[16, 16]], 2 * C, 0, False)
-            for b in range(3):
+            for b in range(4):
                 unit(b)
             mask(1, 0)
+            tt(A("cx", 0, 16), A("ctmp"), A("ceq", 0, 16), ALU.add)
         hold(0, 0)
-        if t:
-            mask(1, 0)
-        equal(0, 0)
         hold(1, 0)
+        equal(0, 0)
+        equal(1, 0)
         mask(0, 1)
         mask(1, 1)
-        equal(1, 0)
-        hold(0, 1)
-        hold(1, 1)
 
         def compare(c):
             s = A("sc", C + 16 * c + 15, C + 16 * c + 16)
@@ -368,6 +378,10 @@ def rank_program(g, core, T, topo):
 
         def total(out, flags, c, init):
             scan(A(out, H * c, H * c + H), A(flags, C * c, C * c + H), A(flags, C * c + H, C * c + C), init, ALU.add, ALU.add)
+
+        compare(0)
+        hold(0, 1)
+        hold(1, 1)
 
         for k in range(2):
             for h in range(2):
@@ -380,12 +394,12 @@ def rank_program(g, core, T, topo):
                 if e < C:
                     act(A("sg", C * c + e, C * c + C), A("sg", C * c + e, C * c + C), ACT.Relu, scale=-1.0, accum=A("accg", c, c + 1))
 
-        for c in range(16):
+        for c in range(1, 16):
             compare(c)
-            if c == 0:
+            if c == 1:
                 equal(0, 1)
                 equal(1, 1)
-            if c == 1:
+            if c == 2:
                 scan(A("eqs"), A("ceq"), A("eqf"), 0.0, ALU.mult, ALU.subtract)
         for c in range(16):
             total("sa", "fa", c, A("eqs", C + 16 * c + 15, C + 16 * c + 16))
@@ -395,60 +409,64 @@ def rank_program(g, core, T, topo):
             ts(A("khi", e, 16), A("klo", e, 16), float(C), ALU.add)
         tt(A("dd", 0, 8), A("accg", 0, 8), A("accl", 0, 8), ALU.subtract)
         tt(A("ke"), A("eqs", 15, C, 16), A("khi" if hi else "klo"), ALU.add)
-        ts(ra_own, A("sa", H - 1, 16 * H, H), float(oo), ALU.add)
-        send(t, hi, [3])
-        if t == 0:
-            unit(3)
+        ts(L("ra", oo), A("sa", H - 1, 16 * H, H), 0.0, ALU.add)
+        send(t, "ra")
 
-        arrive(t, hi, [0, 1])
-        arrive(t, hi, [2])
-        mm(3, "upq", "ups", 128, tq, tsc, C, C)
+        for h in range(2):
+            arrive(t, "codes%d" % h)
+            arrive(t, "scales%d" % h)
+            mm((3, 0)[h], "upq", "ups", 128, tq, tsc, C + H * h, H)
         mm(7, "upq", "ups", 128, tq, tsc, C, C)
         for c in range(e, 16):
             act(A("sgx", C * c, C * c + C), A("p7", 0, C), ACT.Sign, bias=A("sc", 16 * c + 15, 16 * c + 16), scale=-1.0)
         for c in range(e, 16):
             act(A("sgx", C * c, C * c + C), A("sgx", C * c, C * c + C), ACT.Relu, scale=1.0 if hi else -1.0, accum=A("accx", c, c + 1))
-
         if t == 0:
             for k in range(4):
                 act(A("cx", 16 << k, 32 << k), A("cx", 0, 16 << k), ACT.Copy)
 
-        def against(c):
-            ts(A("fb", C * c, C * c + C), A("p3", 0, C), A("sc", 16 * c + 15, 16 * c + 16), ALU.is_ge if hi else ALU.is_gt)
+        def against(c, h):
+            ts(A("fb", C * c + H * h, C * c + H * h + H), A("p%d" % (3, 0)[h], 0, H), A("sc", 16 * c + 15, 16 * c + 16), ALU.is_ge if hi else ALU.is_gt)
 
         def place(c):
             total("sx", "fb", c, A("own", c, c + 1))
 
+        def ordered(a, b):
+            scatter(A("inva"), L("ra", oo, a, b), A("iotaj", oo + 16 * a, oo + 16 * b))
+
+        against(0, 0)
         tt(A("own", 0, 8), A("dd", 0, 8), A("ke", 0, 8), ALU.add)
-        for c in range(9):
-            against(c)
-        for c in range(8):
+        for c in range(1, FIRST + 1):
+            against(c, 0)
+        for c in range(FIRST + 1):
+            against(c, 1)
+        for c in range(FIRST):
             place(c)
-        against(9)
-        ts(A(lb, 16 * hi, 16 * hi + 8), A("sx", H - 1, 8 * H, H), float(C), ALU.add)
-        send(t, hi, [4])
+        against(9, 0)
+        against(9, 1)
+        ts(L("rb", oo, 0, FIRST), A("sx", H - 1, FIRST * H, H), float(C), ALU.add)
+        send(t, "rb0")
         tt(A("dd", 8, 16), A("accg", 8, 16), A("accl", 8, 16), ALU.subtract)
-        against(10)
+        against(10, 0)
+        against(10, 1)
         tt(A("own", 8, 16), A("dd", 8, 16), A("ke", 8, 16), ALU.add)
         for c in range(11, e):
-            against(c)
-        for c in range(8, e - 2):
+            against(c, 0)
+            against(c, 1)
+        for c in range(FIRST, e):
             place(c)
-        tt(A("rbm", e, 16), A("own", e, 16), A("accx", e, 16), ALU.subtract if hi else ALU.add)
-        for c in range(e - 2, e):
-            place(c)
-        ts(A(lb, 16 * hi + e, 16 * hi + 16), A("rbm", e, 16), float(C), ALU.add)
-        ts(A(lb, 16 * hi + 8, 16 * hi + e), A("sx", H * 8 + H - 1, H * e, H), float(C), ALU.add)
-        send(t, hi, [5])
-        if t == 0:
-            quant(A("eq4"), A("es"), A("eb"))
+        tt(A("dd", e, 16), A("own", e, 16), A("accx", e, 16), ALU.subtract if hi else ALU.add)
+        ordered(0, 2)
+        ts(L("rb", oo, FIRST, e), A("sx", H * FIRST + H - 1, H * e, H), float(C), ALU.add)
+        ts(L("rb", oo, e, 16), A("dd", e, 16), float(C), ALU.add)
+        send(t, "rb1")
 
-        banks, banks2 = [4, 0, 1, 6], [5, 2, 3, 7]
+        banks, banks2 = [4, 1, 6, 0], [5, 2, 3, 7]
 
-        def mates(inv, o, ra):
-            copy(A("invs", o, o + C, 2), A(inv, o + 1, o + C, 2))
-            copy(A("invs", o + 1, o + C, 2), A(inv, o, o + C, 2))
-            act(A("arep", o, o + C), G(A("invs", 0, o + C), ra), ACT.Copy)
+        def mates(inv, o):
+            act(A("invs", o, o + C, 2), A(inv, 1, C, 2), ACT.Copy)
+            act(A("invs", o + 1, o + C, 2), A(inv, 0, C, 2), ACT.Copy)
+            act(A("arep", o, o + C), G(A("invs", o, o + C), L("ra", o)), ACT.Copy)
 
         def halved(b):
             act(A("dpp", C * b, C * b + C), A("p%d" % banks[b], C, 2 * C), ACT.Copy, scale=0.5)
@@ -461,56 +479,57 @@ def rank_program(g, core, T, topo):
 
         def unpacked(b, own):
             if own:
-                act(A("dp", 384 * b, 384 * b + C), A("p%d" % banks[b], 0, C), ACT.Copy)
+                act(A("dp", 384 * b + H, 384 * b + 384), A("p%d" % banks[b], 0, C), ACT.Copy)
             else:
-                act(A("dp", 384 * b + C, 384 * b + 384), A("p%d" % banks2[b], 1, C, 2), ACT.Copy)
+                act(A("dp", 384 * b, 384 * b + H), A("p%d" % banks2[b], 1, C, 2), ACT.Copy)
 
-        def mate_list(o, step):
-            if step == 0:
-                wrap(("xs3", o), C, A("arep", o, o + C))
-            else:
-                unwrap(A("awl", o // 16, o // 16 + 16), ("xs3", o), C, C - o)
+        def numbers():
+            for b in range(4):
+                mm(banks[b], "eq4", "es", 128 * b, tq, tsc, 0, 2 * C)
+            unpacked(0, True)
+            halved(0)
 
-        for b in range(4):
-            mm(banks[b], "eq4", "es", 128 * b, tq, tsc, 0, 2 * C)
-        for b in range(2):
-            halved(b)
-            unpacked(b, True)
-        arrive(t, hi, [3])
-        scatter(A("inva", 0, oo + C), ra_own, A("iotaj", oo, oo + C))
-        scatter(A("inw", 0, po + C), A(msg, 16 * (1 - hi), 16 * (1 - hi) + 8), A("iotaj", po, po + H))
-        mates("inva", oo, ra_own)
-        scatter(A("inw", 0, po + C), A(msg, 16 * (1 - hi) + 8, 16 * (1 - hi) + 16), A("iotaj", po + H, po + C))
+        if t:
+            numbers()
+        ordered(2, 16)
+        mates("inva", oo)
+        arrive(t, "ra")
+        scatter(A("inw"), L("ra", po), A("iotaj", po, po + C))
+        mates("inw", po)
         if t == 0:
-            ts(A("cw"), A("cw0"), A("rf", 0, 1), ALU.add)
+            quant(A("eq4"), A("es"), A("eb"))
+            numbers()
+        for b in range(1, 4):
+            halved(b)
+        unpacked(1, True)
+        scatter(A("mm"), L("rb", oo), A("arep", oo, oo + C))
+        wrap(("xs4", 0), C, A("inw"))
+        arrive(t, "rb0")
+        scatter(A("mm"), L("rb", po, 0, FIRST), A("arep", po, po + 16 * FIRST))
+        unwrap(A("inl"), ("xs4", 0), C, C - po)
+        picked(0)
+        picked(1)
+
+        arrive(t, "rb1")
+        scatter(A("mm"), L("rb", po, FIRST, 16), A("arep", po + 16 * FIRST, po + C))
+        if t == 0:
             copy(A("cx2", 0, C, 2), A("cx", 0, H))
+            ts(A("cw"), A("cw0"), A("rf", 0, 1), ALU.add)
         if t == 1:
             quant(A("vq"), A("vs"), A("vb"))
-        mates("inw", po, ra_par)
-        halved(2)
-        halved(3)
-        wrap(("xs4", 0), C, A("inw", po, po + C))
-        scatter(A("mm"), A(lb, 16 * hi, 16 * hi + 16), A("arep", oo, oo + C))
-        unwrap(A("inl"), ("xs4", 0), C, C - po)
-        for b in range(3):
-            picked(b)
-        arrive(t, hi, [4])
-        scatter(A("mm"), A(lb, 16 * (1 - hi), 16 * (1 - hi) + 8), A("arep", po, po + H))
-        mate_list(oo, 0)
-
-        arrive(t, hi, [5])
-        scatter(A("mm"), A(lb, 16 * (1 - hi) + 8, 16 * (1 - hi) + 16), A("arep", po + H, po + C))
-        mate_list(oo, 1)
         copy(A("ms", 0, 512, 2), A("mm", 1, 512, 2))
         copy(A("ms", 1, 512, 2), A("mm", 0, 512, 2))
-        mate_list(po, 0)
+        mean(0)
         P, low, twin = ["pa", "pb"], ["lowa", "lowb"], ["lowc", "lowd"]
         side = (po, oo)
 
-        def square(k, h):
+        def square(k, h, vector=False):
             o = side[h]
-            was = G(A(P[1 - k % 2]), A("ll", 32 * k + o // 16 - 32, 32 * k + o // 16 - 16)) if k else G(A("ms"), A(lb, o // 16, o // 16 + 16))
-            act(A(P[k % 2], o, o + C), was, ACT.Copy)
+            was = G(A(P[1 - k % 2]), A("ll", 32 * k + o // 16 - 32, 32 * k + o // 16 - 16)) if k else G(A("ms"), L("rb", o))
+            if vector:
+                copy(A(P[k % 2], o, o + C), was)
+            else:
+                act(A(P[k % 2], o, o + C), was, ACT.Copy)
 
         def held(k, h):
             wrap(("xs" if k % 2 else "xs2", side[h]), C, A(P[k % 2], side[h], side[h] + C))
@@ -525,92 +544,121 @@ def rank_program(g, core, T, topo):
             else:
                 scan(A(low[0], a, b), A("iotaj", a, b), A(P[0], a, b), -1024.0, ALU.max, ALU.min)
 
-        def again(k, h, a=0, b=C, vector=False):
+        def again(k, h, a=0, b=C, by="scalar"):
             a, b = side[h] + a, side[h] + b
-            if a < b and vector:
+            if by == "vector":
                 copy(A(twin[k % 2], a, b), A(low[k % 2], a, b))
-            elif a < b:
+            elif by == "pool":
+                keep(A(twin[k % 2], a, b), A(low[k % 2], a, b), b - a)
+            else:
                 act(A(twin[k % 2], a, b), A(low[k % 2], a, b), ACT.Copy)
 
-        copy(A(P[0], po, po + C), G(A("ms"), A(lb, po // 16, po // 16 + 16)))
+        square(0, 0, True)
         square(0, 1)
-        picked(3)
-        mate_list(po, 1)
+        picked(2)
+        wrap(("xs3", 0), C, A("arep", oo, oo + C))
         held(0, 0)
-        least(0, 0)
-        listed(0, 0)
         held(0, 1)
-        square(1, 0)
         least(0, 1)
+        listed(0, 0)
         listed(0, 1)
         square(1, 1)
-        again(0, 0, vector=True)
-        again(0, 1, vector=True)
-        mean(0)
+        picked(3)
+        unpacked(2, True)
+        least(0, 0)
+        square(1, 0, True)
+        again(0, 1, by="pool")
+        again(0, 0, by="vector")
         held(1, 0)
-        mean(1)
-        listed(1, 0)
+        unwrap(L("am", oo), ("xs3", 0), C, C - oo)
+        send(t, "am")
         held(1, 1)
-        mean(2)
+        listed(1, 0)
+        mean(1)
         listed(1, 1)
         for k in range(1, DOUBLINGS - 1):
             square(k + 1, 0)
-            if k > 1:
-                again(k - 1, 1, 0, H)
             square(k + 1, 1)
             least(k, 0)
             again(k, 0)
+            if k == 1:
+                least(k, 1, H, C)
+                again(k, 1, H, C, "pool")
             held(k + 1, 0)
             least(k, 1, 0, H)
+            if k < DOUBLINGS - 2:
+                again(k, 1, 0, H)
             listed(k + 1, 0)
-            least(k, 1, H, C)
             held(k + 1, 1)
-            again(k, 1, H, C, True)
+            if k > 1:
+                least(k, 1, H, C)
+            if 1 < k < DOUBLINGS - 2:
+                again(k, 1, H, C, "pool")
+            if k < 3:
+                mean(k + 1)
             listed(k + 1, 1)
         k = DOUBLINGS - 1
-        again(k - 1, 1, 0, H)
+        again(k - 1, 1)
         least(k, 0)
-        unpacked(2, True)
         unpacked(3, True)
         again(k, 0)
         least(k, 1)
         again(k, 1)
-        mean(3)
-
-        lw, tw = low[1 - DOUBLINGS % 2], twin[1 - DOUBLINGS % 2]
-
-        def fl(h, shift):
-            return A("fl", 16 + 272 * h - shift, 272 + 272 * h - shift)
-
-        def flags(h):
-            tt(fl(h, 0), G(A(lw, C * h, C * h + C), A("awl", 16 * h, 16 * h + 16)), A(tw, C * h, C * h + C), ALU.is_gt)
-
-        flags(1 - hi)
-        act(A("fa1"), fl(1 - hi, 0), ACT.Copy, scale=129.0)
-        flags(hi)
-        ts(A("fb1", 16, 272), fl(1 - hi, 0), -128.0, ALU.mult)
         quant(A("bq"), A("bs"), A("bt"))
         for b in range(4):
             mm(banks2[b], "eq4", "es", 128 * b, "bq", "bs", 0, C)
-            unpacked(b, False)
-        scan(A("sp"), A("fa1"), A("fb1", 15, 271), 0.0, ALU.add, ALU.add)
-        scan(A("vv"), fl(hi, 0), fl(hi, 1), 0.0, ALU.add, ALU.add)
-        copy(A("ge"), G(A("sp"), A("inl")))
-        wrap(("xs6", 0), H, A("vv", 0, H))
-        scan(A("xs5"), A("cx2"), A("ge"), 0.0, ALU.mult, ALU.max)
-        wrap(("xs6", H), H, A("vv", H, C))
-        ts(A("kl"), A("xs5", 31, C, 32), A("scl2", 0, 1), ALU.mult, -257.0, ALU.add)
-        unwrap(A("lu", 0, 8), ("xs6", 0), H, 0)
-        scatter(A("wn"), A("kl"), A("iotaj", C, C + H))
-        unwrap(A("lu", 8, 16), ("xs6", H), H, 0)
-        for h in range(2):
-            tt(A("yv", H * h, H * h + H), G(A("wn"), A("lu", 8 * h, 8 + 8 * h)), A("iotaj", H * h, H * h + H), ALU.max)
-        for h in range(2):
-            wrap(("xs7", H * h), H, A("yv", H * h, H * h + H))
-        for h in range(2):
-            unwrap(A("yl", 8 * h, 8 * h + 8), ("xs7", H * h), H, C)
 
-        nq, nsc = "tq%d" % (t + 1), "ts%d" % (t + 1)
+        lw, tw = low[1 - DOUBLINGS % 2], twin[1 - DOUBLINGS % 2]
+
+        def fl(o, shift=0):
+            return A("fl", 16 + 272 * o // C - shift, 272 + 272 * o // C - shift)
+
+        def flags(o, a=0, b=C):
+            f = 16 + 272 * o // C
+            tt(A("fl", f + a, f + b), G(A(lw, o, o + C), L("am", o, a // 16, b // 16)), A(tw, o + a, o + b), ALU.is_gt)
+
+        reds = []
+        if last:
+            reds = [lambda: unwrap(A("wi"), ("xs6", 0), C, 1), lambda: ts(A("nf"), A("wi"), 1, ALU.bitwise_and),
+                    lambda: ts(A("hh"), A("wi"), 1, ALU.arith_shift_right), lambda: tt(A("tc"), A("nf"), A("cw"), ALU.mult),
+                    lambda: tt(A("lm"), A("tc"), A("hh"), ALU.max), lambda: copy(A("ol16"), A("lm"))]
+
+        def red():
+            if reds:
+                reds.pop(0)()
+
+        arrive(t, "am")
+        flags(po)
+        act(A("fa1"), fl(po), ACT.Copy, scale=129.0)
+        unpacked(0, False)
+        unpacked(1, False)
+        flags(oo, 0, H)
+        ts(A("fb1", 16, 272), fl(po), -128.0, ALU.mult)
+        flags(oo, H, C)
+        scan(A("sp"), A("fa1"), A("fb1", 15, 271), 0.0, ALU.add, ALU.add)
+        scan(A("vv"), fl(oo), fl(oo, 1), 0.0, ALU.add, ALU.add)
+        act(A("ge", H, C), G(A("sp"), A("inl", 8, 16)), ACT.Copy)
+        copy(A("ge", 0, H), G(A("sp"), A("inl", 0, 8)))
+        unpacked(2, False)
+        unpacked(3, False)
+        wrap(("xs6", 0), C, A("vv"))
+        scan(A("xs5"), A("cx2"), A("ge"), 0.0, ALU.mult, ALU.max)
+        unwrap(A("lu", 0, 8), ("xs6", 0), H, 0)
+        red()
+        ts(A("kl"), A("xs5", 31, C, 32), A("scl2", 0, 1), ALU.mult, -257.0, ALU.add)
+        unwrap(A("lu", 8, 16), ("xs6", H), H, 0)
+        red()
+        red()
+        scatter(A("wn"), A("kl"), A("iotaj", 0, H))
+        red()
+        for h in range(2):
+            tt(A("yv", H * h, H * h + H), G(A("wn"), A("lu", 8 * h, 8 * h + 8)), A("iotaj", H + H * h, C + H * h), ALU.min)
+        wrap(("xs7", 0), H, A("yv", 0, H))
+        red()
+        wrap(("xs7", H), H, A("yv", H, C))
+        unwrap(A("yl", 0, 8), ("xs7", 0), H, C)
+        red()
+        unwrap(A("yl", 8, 16), ("xs7", H), H, C)
 
         def part(h, b, vector):
             win = G(A("dp", 384 * b, 384 * b + 384), A("yl", 8 * h, 8 * h + 8))
@@ -622,75 +670,43 @@ def rank_program(g, core, T, topo):
         def packed(h):
             quant(A("zq", H * h, H * h + H), A("zs", H * h, H * h + H), A("yt", 4 * H * h, 4 * H * (h + 1)))
 
-        def products(h, bs):
-            for b in bs:
-                mm(b, "wq", "wsc", 128 * b, "zq", "zs", H * h, H)
-            for b in bs:
-                mm(4 + b, "eq4", "es", 128 * b, "zq", "zs", H * h, H)
-
-        def relu(h, b, vector=False):
-            if vector:
-                ts(A("rr", C * b + H * h, C * b + H * h + H), A("p%d" % b, 0, H), 0.0, ALU.max, 0.03125, ALU.mult)
-            else:
-                act(A("rr", C * b + H * h, C * b + H * h + H), A("p%d" % b, 0, H), ACT.Relu, scale=0.03125)
+        def products(h):
+            for b in (0, 4, 1, 2, 3, 5, 6, 7):
+                mm(b, "wq" if b < 4 else "eq4", "wsc" if b < 4 else "es", 128 * (b % 4), "zq", "zs", H * h, H)
 
         def new(h, b):
+            act(A("rr", C * b + H * h, C * b + H * h + H), A("p%d" % b, 0, H), ACT.Relu, scale=0.03125)
             tt(A("xn", 4 * H * h + b, 4 * H * (h + 1), 4), A("p%d" % (4 + b), 0, H), A("rr", C * b + H * h, C * b + H * h + H), ALU.add)
 
-        def state(h):
-            quant(A(nq, H * h, H * h + H), A(nsc, H * h, H * h + H), A("xn", 4 * H * h, 4 * H * (h + 1)))
-
-        reds = []
-        if last:
-            reds = [lambda: unwrap(A("wi"), ("xs6", 0), C, 1), lambda: ts(A("nf"), A("wi"), 1, ALU.bitwise_and),
-                    lambda: ts(A("hh"), A("wi"), 1, ALU.arith_shift_right), lambda: tt(A("tc"), A("nf"), A("cw"), ALU.mult),
-                    lambda: tt(A("lm"), A("tc"), A("hh"), ALU.max), lambda: copy(A("ol16"), A("lm"))]
-
-        def red(n=1):
-            for k in range(n):
-                if reds:
-                    reds.pop(0)()
-
-        for b in range(3):
-            red()
-            part(0, b, True)
+        part(0, 2, False)
         part(0, 3, False)
-        red()
+        part(0, 0, True)
+        part(0, 1, True)
         part(1, 0, True)
-        red()
         packed(0)
-        products(0, range(4))
-        part(1, 2, False)
+        products(0)
         part(1, 3, False)
-        red()
+        part(1, 2, False)
         part(1, 1, True)
-        if last:
-            scatter(A("wo"), A("ol16", 0, 8), A("iotaj", C, C + H))
         packed(1)
         for b in range(4):
-            relu(0, b, b < 2)
-        for b in range(4):
             new(0, b)
-        products(1, (0, 1))
-        products(1, (2, 3))
-        state(0)
-        if last:
-            results(0)
-        else:
-            send(t + 1, 1 if rank & STEP[t + 1] else 0, [0])
+        products(1)
+        state(t + 1, 0)
         for b in range(4):
-            relu(1, b)
             new(1, b)
             if b == 1 and not last:
                 scores(t + 1, 0)
         if last:
-            scatter(A("wo"), A("ol16", 8, 16), A("iotaj", C + H, 2 * C))
-            dma("sync", T.ol[:, :], T.wo[0:128:16, 1:129], [A("wo")], [])
+            result(0)
         else:
             mask(0, 0)
-        state(1)
+            mask(1, 0)
+        state(t + 1, 1)
 
-    results(1)
+    result(1)
     for k in range(4):
         dma("sync", T.osc[4 * k:4 * k + 4, :], T["ts%d" % ROUNDS][32 * k:32 * k + 4, 0:C], [A("ts%d" % ROUNDS)], [])
+    scatter(A("wo"), A("ol16"), A("iotaj", C, 2 * C))
+    dma("sync", T.ol[:, :], T.wo[0:128:16, 1:129], [A("wo")], [])
     emit(g, T, ops, left[0])

from concourse.bass import DstId, RemoteDMATransfer
from concourse.mybir import dt, AluOpType, ActivationFunctionType

ALU = AluOpType
ACT = ActivationFunctionType
C = 256
H = C // 2
ROUNDS = 3
STEP = [1, 2, 4]
DOUBLINGS = 8
CROSS_S = 4
FIRST = 8
BIG = 2.0 ** 40
Q4, U8, BF, F32, I32, U16 = "float8_e4m3fn_x4", "uint8", "bfloat16", "float32", "int32", "uint16"

SCRATCH = {}
for _d, _l in [
    (BF, "x0 1024 xn 1024 ub 512 vb 512 ones 512 eb 2048 t16 512 maskd 128 ceq 512 c0 128 cx 256 ctmp 16 iotaj 512 "
         "cx2 256 wn 272 eqf 512 eqs 512 fa 4096 fb 4096 sa 2048 sx 2048 sg 4096 sgx 4096 inva 256 inw 256 invs 512 "
         "arep 512 xs 512 xs2 512 xs3 256 xs4 256 xs5 256 xs6 256 xs7 256 mm 512 ms 512 pa 512 pb 512 lowa 512 lowb 512 lowc 512 lowd 512 "
         "fl 544 vv 256 fa1 256 fb1 272 sp 256 ge 256 yv 256 yw 128 dp 1536 dpp 1024 g1 1024 bt 1024 alt 256 yt 1024"),
    (Q4, "uq 128 upq 256 vq 128 wq 512 eq4 512 bq 256 zq 256 tq0 512 tq1 512 tq2 512 tq3 256"),
    (U8, "us 128 ups 256 vs 128 wsc 512 es 512 bs 256 zs 256 ts0 512 ts1 512 ts2 512 ts3 256"),
    (I32, "pcol 8 rcol 8 offi 16 cw0 16 cw 16 wi 16 hh 16 nf 16 tc 16 lm 16"),
    (F32, "rf 8 rf1 8 scl 8 scl2 8 klo 16 khi 16 wo 768 sm 512 sc 512 accl 16 accg 16 accx 16 ke 16 dd 16 own 16 rr 1024 yo 256"),
    (U16, "offu 16 inl 16 ll 256 lu 16 kl 8 yl 16 ol16 16 ra 96 rb 96 am 96"),
]:
    _w = _l.split()
    for _i in range(0, len(_w), 2):
        SCRATCH[_w[_i]] = ("sbuf", [128, int(_w[_i + 1])], _d)
for _b in range(8):
    SCRATCH["p%d" % _b] = ("psum", [128, 512], F32)

SEMAPHORES = ["s_vector", "s_scalar", "s_tensor", "s_pool", "left"] + ["dma%d" % _k for _k in range(20)]
for _t in range(ROUNDS):
    SEMAPHORES += [_n + str(_t) for _n in ("codes0", "codes1", "scales0", "scales1", "ra", "rb0", "rb1", "am")]


def _mask(engines):
    m = 0
    for e in engines:
        m |= 1 << e
    return m


def relays(T, topo, src, dst):
    r = [c for c in topo.cores_of(src) if c != src and T.rank_of(c) is None and topo.may_write(c, dst)]
    r.sort(key=lambda c: (topo.die(c) != topo.die(src), c))
    return r[:4]


def messages(t, hi):
    out = {}
    for h in range(2):
        cuts = [H * h + H // 2 * k for k in range(2)]
        out["codes%d" % h] = [(h + 2 * k, "tq%d" % t, (a, a + H // 2), (C + a, C + a + H // 2)) for k, a in enumerate(cuts)]
        out["scales%d" % h] = [(1 + h, "ts%d" % t, (H * h, H * h + H), (C + H * h, C + H * h + H))]
    o = 32 * t + 16 * hi
    out["ra"] = [(0, "ra", (o, o + 16), (o, o + 16))]
    out["rb0"] = [(1, "rb", (o, o + FIRST), (o, o + FIRST))]
    out["rb1"] = [(0, "rb", (o + FIRST, o + 16), (o + FIRST, o + 16))]
    out["am"] = [(1, "am", (o, o + 16), (o, o + 16))]
    return out


def view(T, name, cols):
    ap = T[name][:, cols[0]:cols[1]]
    return ap.bitcast(dt.uint8) if SCRATCH[name][2] == Q4 else ap


def relay_program(g, core, T, topo):
    left = 0
    for src in [c for c in topo.cores_of(core) if T.rank_of(c) is not None]:
        r = T.rank_of(src)
        for t in range(ROUNDS):
            dst = T.cores[r ^ STEP[t]]
            rel = relays(T, topo, src, dst)
            for what, ps in messages(t, 1 if r & STEP[t] else 0).items():
                for k, name, a, b in ps:
                    if rel[k] != core:
                        continue
                    sem = T.sem[what + str(t)]
                    g.wait_ge(sem, len(topo.engines(src, core)) // len(ps))
                    rid, pid = topo.addr(dst, core)
                    g.remote_dma(view(T, name, b), view(T, name, b), sem, T.sem.left, pid, rid, topo.mask(core, dst))
                    left += len(topo.engines(core, dst))
    if left:
        g.wait_ge(T.sem.left, left)


def clash(a, b):
    if a[2] <= b[1] or b[2] <= a[1]:
        return False
    return not (a[3] > 1 and a[3] == b[3] and a[1] % a[3] != b[1] % b[3])


def emit(g, T, ops, left):
    queues = {"vector": g.vector, "scalar": g.scalar, "tensor": g.tensor, "pool": g, "sync": g.sync}
    seen = {}
    lines = {q: [] for q in queues}
    for i, o in enumerate(ops):
        deps = set()
        regs = [(r, False) for r in o["r"]] + [(r, True) for r in o["w"]]
        for reg, wr in regs:
            bank = SCRATCH[reg[0]][0] == "psum"
            for j, reg2, wr2 in seen.get(reg[0], []):
                if (wr or wr2 or ops[j]["q"] != o["q"]) if bank else ((wr or wr2) and clash(reg, reg2)):
                    deps.add(j)
        for reg, wr in regs:
            seen.setdefault(reg[0], []).append((i, reg, wr))
        o["deps"] = deps
        if o["kind"] == "c":
            o["pos"] = len(lines[o["q"]])
            lines[o["q"]].append(i)
    waited = {q: {} for q in queues}
    for o in ops:
        o["waits"] = []
        if o["kind"] == "arrive":
            continue
        want = {}
        for j in o["deps"]:
            p = ops[j]
            if p["kind"] == "c":
                want[p["q"]] = max(want.get(p["q"], -1), p["pos"])
            elif p["kind"] in ("dma", "arrive"):
                want[("x", j)] = 0
        for key in sorted(want, key=str):
            pos = want[key]
            if waited[o["q"]].get(key, -1) >= pos:
                continue
            if key == o["q"] and o["kind"] == "c":
                k, span = o["pos"] - 1, 0
                while k > pos and span < 600:
                    span += sum(max(64, (r[2] - r[1]) // r[3] // 2) for r in ops[lines[key][k]]["w"][:1])
                    k -= 1
                pos = k
            waited[o["q"]][key] = pos
            j = key[1] if isinstance(key, tuple) else lines[key][pos]
            ops[j]["inc"] = True
            o["waits"].append(j)
    count = {q: 0 for q in queues}
    ndma = 0
    for o in ops:
        if o["kind"] == "c" and o.get("inc"):
            count[o["q"]] += 1
            o["sem"], o["val"] = "s_" + o["q"], count[o["q"]]
        elif o["kind"] == "dma":
            o["sem"], o["val"] = "dma%d" % ndma, 16
            ndma += 1
    for o in ops:
        if o["kind"] == "arrive":
            continue
        q = queues[o["q"]]
        for j in o["waits"]:
            q.wait_ge(T.sem[ops[j]["sem"]], ops[j]["val"])
        ins = o["f"](q)
        if o["kind"] == "dma":
            ins.then_inc(T.sem[o["sem"]], 16)
        elif o["kind"] == "c" and o.get("inc"):
            ins.then_inc(T.sem[o["sem"]], 1)
    for o in ops:
        if o["kind"] == "dma" and not o.get("inc"):
            queues[o["q"]].wait_ge(T.sem[o["sem"]], 16)
    g.wait_ge(T.sem.left, left)


def rank_program(g, core, T, topo):
    rank = T.rank_of(core)
    if rank is None:
        relay_program(g, core, T, topo)
        return
    ops = []
    left = [0]

    def A(name, a=0, b=None, step=1):
        if b is None:
            b = SCRATCH[name][1][1]
        return (T[name][:, a:b:step] if step > 1 else T[name][:, a:b], [(name, a, b, step)])

    def G(win, off):
        return (win[0].indirect(off[0]), win[1] + off[1])

    def add(q, f, r, w, kind="c"):
        ops.append({"q": q, "f": f, "r": [x for a in r if isinstance(a, tuple) for x in a[1]], "w": [x for a in w for x in a[1]], "kind": kind})

    def ap(a):
        return a[0] if isinstance(a, tuple) else a

    def copy(out, in_):
        add("vector", lambda q: q.tensor_copy(out[0], in_[0]), [in_], [out])

    def scatter(win, off, in_):
        add("vector", lambda q: q.tensor_copy(win[0].indirect(off[0]), in_[0]), [in_, off], [win])

    def tt(out, a, b, op):
        add("vector", lambda q: q.tensor_tensor(out[0], a[0], b[0], op), [a, b], [out])

    def ts(out, a, s1, op0, s2=None, op1=None):
        if op1 is None:
            add("vector", lambda q: q.tensor_scalar(out[0], a[0], ap(s1), None, op0), [a, s1], [out])
        else:
            add("vector", lambda q: q.tensor_scalar(out[0], a[0], ap(s1), ap(s2), op0, op1), [a, s1, s2], [out])

    def scan(out, d0, d1, init, op0, op1):
        add("vector", lambda q: q.tensor_tensor_scan(out[0], d0[0], d1[0], ap(init), op0, op1), [d0, d1, init], [out])

    def memset(out, v):
        add("vector", lambda q: q.memset(out[0], v), [], [out])

    def quant(cq, cs, in_):
        add("vector", lambda q: q.quantize_mx(cq[0], cs[0], in_[0]), [in_], [cq, cs])

    def act(out, in_, func, bias=None, scale=None, accum=None):
        kw = {}
        if bias is not None:
            kw["bias"] = ap(bias)
        if scale is not None:
            kw["scale"] = scale
        if accum is not None:
            kw["accum_out"] = accum[0]
        add("scalar", lambda q: q.activation(out[0], in_[0], func, **kw), [in_, bias], [out] + ([accum] if accum else []))

    def mm(bank, lq, ls, la, rq, rs, ra, n):
        out = A("p%d" % bank, 0, n)
        a, b, c, d = A(lq, la, la + 128), A(ls, la, la + 128), A(rq, ra, ra + n), A(rs, ra, ra + n)
        add("tensor", lambda q: q.matmul_mx(out[0], a[0], b[0], c[0], d[0], True, True), [a, b, c, d], [out])

    def iota(out, pattern, base, cm, small=True):
        if small:
            add("pool", lambda q: q.iota(out[0], pattern, base, cm, allow_small_or_imprecise_dtypes=True), [], [out])
        else:
            add("pool", lambda q: q.iota(out[0], pattern, base, cm), [], [out])

    def unit(b):
        out = A("eb", 512 * b, 512 * b + 512)
        add("pool", lambda q: q.affine_select(out[0], T.ones[:], [[-1, 512]], ALU.is_equal, 0.0, b, 4), [A("ones")], [out])

    def keep(out, in_, n):
        add("pool", lambda q: q.affine_select(out[0], in_[0], [[0, n]], ALU.is_ge, 0.0, 0, 0), [in_], [out])

    def dma(queue, out, in_, r, w):
        add(queue, lambda q: q.dma_start(out, in_), r, w, "dma")

    def send(t, what):
        rel = relays(T, topo, core, T.cores[rank ^ STEP[t]])
        ps = messages(t, 1 if rank & STEP[t] else 0)[what]
        trs = []
        for i, (k, name, a, b) in enumerate(ps):
            eng = topo.engines(core, rel[k])
            n = len(eng) // len(ps)
            rid, pid = topo.addr(rel[k], core)
            trs.append((view(T, name, b), view(T, name, a), pid, rid, _mask(eng[n * i:n * i + n])))
            left[0] += n
        sem = T.sem[what + str(t)]
        if len(ps) > 1:
            fused = [RemoteDMATransfer(dst_ids=[DstId(rid=rid, pnc=pid)], dma_engine_mask=m, remote_sem=sem, src=a, dst=b)
                     for b, a, pid, rid, m in trs]
            add("pool", lambda q: q.remote_dma_fused(fused, local_sem=T.sem.left), [A(p[1], *p[2]) for p in ps], [], "send")
        else:
            b, a, pid, rid, m = trs[0]
            add("pool", lambda q: q.remote_dma(b, a, sem, T.sem.left, pid, rid, m), [A(p[1], *p[2]) for p in ps], [], "send")

    def arrive(t, what):
        rel = relays(T, topo, T.cores[rank ^ STEP[t]], core)
        ps = messages(t, 0 if rank & STEP[t] else 1)[what]
        ops.append({"q": None, "kind": "arrive", "r": [], "w": [(p[1], p[3][0], p[3][1], 1) for p in ps], "sem": what + str(t),
                    "val": sum(len(topo.engines(rel[p[0]], core)) for p in ps)})

    def wrap(tmp, n, src):
        scan(A(tmp[0], tmp[1], tmp[1] + n), A("cx", 0, n), src, 0.0, ALU.mult, ALU.add)

    def unwrap(out, tmp, n, plus):
        ts(out, A(tmp[0], tmp[1] + 15, tmp[1] + n, 16), A("scl", 0, 1), ALU.mult, float(plus), ALU.add)

    dma("sync", T.ub[:], T.u[:], [], [A("ub")])
    dma("scalar", T.x0[:, 0:2 * C], T.x[:, 0:2 * C], [], [A("x0", 0, 2 * C)])
    dma("sync", T.x0[:, 2 * C:4 * C], T.x[:, 2 * C:4 * C], [], [A("x0", 2 * C, 4 * C)])
    dma("sync", T.wq[:].bitcast(dt.uint8), T.wc[:], [A("x0")], [A("wq")])
    dma("sync", T.wsc[:], T.ws[:], [], [A("wsc")])
    dma("sync", T.vb[:], T.v[:], [], [A("vb")])
    iota(A("offi"), [[8, 2], [16, 8]], 0, 0, False)
    iota(A("pcol", 0, 1), [[0, 1]], 0, 1, False)
    iota(A("t16"), [[0, 32], [1, 16]], 0, 0)
    iota(A("iotaj"), [[1, 512]], -C, 0)
    memset(A("ones"), 1.0)
    copy(A("offu"), A("offi"))
    ts(A("rcol", 0, 1), A("pcol", 0, 1), 15, ALU.bitwise_and)
    memset(A("accg"), 0.0)
    memset(A("fl"), 0.0)
    copy(A("rf", 0, 1), A("rcol", 0, 1))
    memset(A("wn"), 1024.0)
    memset(A("fb1", 0, 16), 0.0)
    memset(A("cx2", 1, C, 2), 1.0)
    memset(A("alt", 0, C, 2), 0.0)
    memset(A("alt", 1, C, 2), 1.0)
    ts(A("rf1", 0, 1), A("rf", 0, 1), 1.0, ALU.add)
    ts(A("scl", 0, 1), A("rf", 0, 1), 15.0, ALU.is_equal, 1.0 / BIG, ALU.max)
    ts(A("maskd"), A("t16", 0, H), A("rf", 0, 1), ALU.is_equal)
    ts(A("c0"), A("t16", 0, H), 0.0, ALU.not_equal)
    ts(A("ctmp"), A("t16", 0, 16), A("rf1", 0, 1), ALU.is_equal, BIG, ALU.mult)
    quant(A("uq"), A("us"), A("ub"))
    quant(A("tq0", 0, H), A("ts0", 0, H), A("x0", 0, 4 * H))
    add("vector", lambda q: q.tensor_copy(T.upq[:, 0:256].bitcast(dt.uint32), T.uq[:, 0:128].bitcast(dt.uint32).indirect(T.offu[:, 0:16])),
        [A("uq"), A("offu")], [A("upq")])
    add("scalar", lambda q: q.activation(T.ups[:, 0:256], T.us[:, 0:128].indirect(T.offu[:, 0:16]), ACT.Copy),
        [A("us"), A("offu")], [A("ups")])

    def state(t, h):
        quant(A("tq%d" % t, H * h, H * h + H), A("ts%d" % t, H * h, H * h + H), A("xn" if t else "x0", 4 * H * h, 4 * H * (h + 1)))
        if t < ROUNDS:
            send(t, "codes%d" % h)
            send(t, "scales%d" % h)
        else:
            dma("sync", T.oc[:, 4 * H * h:4 * H * (h + 1)], T["tq%d" % t][:, H * h:H * h + H].bitcast(dt.uint8), [A("tq%d" % t, H * h, H * h + H)], [])

    def scores(t, h):
        tq, tsc = "tq%d" % t, "ts%d" % t
        mm((4, 5)[h], "upq", "ups", 128, tq, tsc, H * h, H)
        mm((1, 6)[h], "upq", "ups", 128, tq, tsc, H * h, H)
        mm((0, 2)[h], "upq", "ups", 0, tq, tsc, 0, H * h + H)

    def half(k, h):
        return A("p%d" % ((4, 5), (0, 2))[k][h], H * h * k, H * h * k + H)

    def mask(k, h):
        tt(A("sm", C * k + H * h, C * k + H * h + H), half(k, h), A("maskd"), ALU.mult)

    def hold(k, h):
        o = C * k + H * h
        scan(A("sc", o, o + H), A("c0"), A("sm", o, o + H), 0.0, ALU.mult, ALU.add)

    def equal(k, h):
        o = C * k + H * h
        tt(A("eqf", o, o + H), half(k, h), A("sc", o, o + H), ALU.is_equal)

    def result(h):
        mm(h, "vq", "vs", 0, "tq%d" % ROUNDS, "ts%d" % ROUNDS, H * h, H)
        act(A("yo", H * h, H * h + H), A("p%d" % h, 0, H), ACT.Copy)
        dma("scalar", T.y[:, H * h:H * h + H], T.yo[:, H * h:H * h + H], [A("yo", H * h, H * h + H)], [])

    send(0, "codes0")
    send(0, "scales0")
    scores(0, 0)
    state(0, 1)
    ts(A("ceq"), A("t16"), A("rf", 0, 1), ALU.not_equal)
    ts(A("scl2", 0, 1), A("scl", 0, 1), 2.0, ALU.mult)
    mask(0, 0)
    for t in range(ROUNDS):
        hi = 1 if rank & STEP[t] else 0
        last = t == ROUNDS - 1
        oo, po = C * hi, C * (1 - hi)
        tq, tsc = "tq%d" % t, "ts%d" % t

        def L(name, o, a=0, b=16):
            return A(name, 32 * t + o // 16 + a, 32 * t + o // 16 + b)

        scores(t, 1)
        if t == 0:
            iota(A("klo"), [[16, 16]], 16 - C, 0)
            iota(A("cw0"), [[16, 16]], 2 * C, 0, False)
            for b in range(4):
                unit(b)
            mask(1, 0)
            tt(A("cx", 0, 16), A("ctmp"), A("ceq", 0, 16), ALU.add)
        hold(0, 0)
        hold(1, 0)
        equal(0, 0)
        equal(1, 0)
        mask(0, 1)
        mask(1, 1)

        def compare(c):
            s = A("sc", C + 16 * c + 15, C + 16 * c + 16)
            e = 16 * c + 16
            ts(A("fa", C * c, C * c + e), A("p2", 0, e), s, ALU.is_ge)
            if e < C:
                ts(A("fa", C * c + e, C * c + C), A("p2", e, C), s, ALU.is_gt)

        def total(out, flags, c, init):
            scan(A(out, H * c, H * c + H), A(flags, C * c, C * c + H), A(flags, C * c + H, C * c + C), init, ALU.add, ALU.add)

        compare(0)
        hold(0, 1)
        hold(1, 1)

        for k in range(2):
            for h in range(2):
                for c in range(8 * k, 8 * k + 8):
                    act(A("sg", C * c + H * h, C * c + H * h + H), A("p%d" % (1, 6)[h], 0, H), ACT.Sign,
                        bias=A("sc", 16 * c + 15, 16 * c + 16), scale=-1.0)
            for c in range(8 * k, 8 * k + 8):
                e = 16 * c + 16
                act(A("sg", C * c, C * c + e), A("sg", C * c, C * c + e), ACT.Relu, accum=A("accl", c, c + 1))
                if e < C:
                    act(A("sg", C * c + e, C * c + C), A("sg", C * c + e, C * c + C), ACT.Relu, scale=-1.0, accum=A("accg", c, c + 1))

        for c in range(1, 16):
            compare(c)
            if c == 1:
                equal(0, 1)
                equal(1, 1)
            if c == 2:
                scan(A("eqs"), A("ceq"), A("eqf"), 0.0, ALU.mult, ALU.subtract)
        for c in range(16):
            total("sa", "fa", c, A("eqs", C + 16 * c + 15, C + 16 * c + 16))
        e = 16 - CROSS_S
        if t == 0:
            copy(A("khi", 0, e), A("klo", 0, e))
            ts(A("khi", e, 16), A("klo", e, 16), float(C), ALU.add)
        tt(A("dd", 0, 8), A("accg", 0, 8), A("accl", 0, 8), ALU.subtract)
        tt(A("ke"), A("eqs", 15, C, 16), A("khi" if hi else "klo"), ALU.add)
        ts(L("ra", oo), A("sa", H - 1, 16 * H, H), 0.0, ALU.add)
        send(t, "ra")

        for h in range(2):
            arrive(t, "codes%d" % h)
            arrive(t, "scales%d" % h)
            mm((3, 0)[h], "upq", "ups", 128, tq, tsc, C + H * h, H)
        mm(7, "upq", "ups", 128, tq, tsc, C, C)
        for c in range(e, 16):
            act(A("sgx", C * c, C * c + C), A("p7", 0, C), ACT.Sign, bias=A("sc", 16 * c + 15, 16 * c + 16), scale=-1.0)
        for c in range(e, 16):
            act(A("sgx", C * c, C * c + C), A("sgx", C * c, C * c + C), ACT.Relu, scale=1.0 if hi else -1.0, accum=A("accx", c, c + 1))
        if t == 0:
            for k in range(4):
                act(A("cx", 16 << k, 32 << k), A("cx", 0, 16 << k), ACT.Copy)

        def against(c, h):
            ts(A("fb", C * c + H * h, C * c + H * h + H), A("p%d" % (3, 0)[h], 0, H), A("sc", 16 * c + 15, 16 * c + 16), ALU.is_ge if hi else ALU.is_gt)

        def place(c):
            total("sx", "fb", c, A("own", c, c + 1))

        def ordered(a, b):
            scatter(A("inva"), L("ra", oo, a, b), A("iotaj", oo + 16 * a, oo + 16 * b))

        against(0, 0)
        tt(A("own", 0, 8), A("dd", 0, 8), A("ke", 0, 8), ALU.add)
        for c in range(1, FIRST + 1):
            against(c, 0)
        for c in range(FIRST + 1):
            against(c, 1)
        for c in range(FIRST):
            place(c)
        against(9, 0)
        against(9, 1)
        ts(L("rb", oo, 0, FIRST), A("sx", H - 1, FIRST * H, H), float(C), ALU.add)
        send(t, "rb0")
        tt(A("dd", 8, 16), A("accg", 8, 16), A("accl", 8, 16), ALU.subtract)
        against(10, 0)
        against(10, 1)
        tt(A("own", 8, 16), A("dd", 8, 16), A("ke", 8, 16), ALU.add)
        for c in range(11, e):
            against(c, 0)
            against(c, 1)
        for c in range(FIRST, e):
            place(c)
        tt(A("dd", e, 16), A("own", e, 16), A("accx", e, 16), ALU.subtract if hi else ALU.add)
        ordered(0, 2)
        ts(L("rb", oo, FIRST, e), A("sx", H * FIRST + H - 1, H * e, H), float(C), ALU.add)
        ts(L("rb", oo, e, 16), A("dd", e, 16), float(C), ALU.add)
        send(t, "rb1")

        banks, banks2 = [4, 1, 6, 0], [5, 2, 3, 7]

        def mates(inv, o):
            act(A("invs", o, o + C, 2), A(inv, 1, C, 2), ACT.Copy)
            act(A("invs", o + 1, o + C, 2), A(inv, 0, C, 2), ACT.Copy)
            act(A("arep", o, o + C), G(A("invs", o, o + C), L("ra", o)), ACT.Copy)

        def halved(b):
            act(A("dpp", C * b, C * b + C), A("p%d" % banks[b], C, 2 * C), ACT.Copy, scale=0.5)

        def picked(b):
            act(A("g1", C * b, C * b + C), G(A("dpp", C * b, C * b + C), A("inl")), ACT.Copy)

        def mean(b):
            scan(A("bt", b, 4 * C, 4), A("alt"), A("g1", C * b, C * b + C), 0.0, ALU.mult, ALU.add)

        def unpacked(b, own):
            if own:
                act(A("dp", 384 * b + H, 384 * b + 384), A("p%d" % banks[b], 0, C), ACT.Copy)
            else:
                act(A("dp", 384 * b, 384 * b + H), A("p%d" % banks2[b], 1, C, 2), ACT.Copy)

        def numbers():
            for b in range(4):
                mm(banks[b], "eq4", "es", 128 * b, tq, tsc, 0, 2 * C)
            unpacked(0, True)
            halved(0)

        if t:
            numbers()
        ordered(2, 16)
        mates("inva", oo)
        arrive(t, "ra")
        scatter(A("inw"), L("ra", po), A("iotaj", po, po + C))
        mates("inw", po)
        if t == 0:
            quant(A("eq4"), A("es"), A("eb"))
            numbers()
        for b in range(1, 4):
            halved(b)
        unpacked(1, True)
        scatter(A("mm"), L("rb", oo), A("arep", oo, oo + C))
        wrap(("xs4", 0), C, A("inw"))
        arrive(t, "rb0")
        scatter(A("mm"), L("rb", po, 0, FIRST), A("arep", po, po + 16 * FIRST))
        unwrap(A("inl"), ("xs4", 0), C, C - po)
        picked(0)
        picked(1)

        arrive(t, "rb1")
        scatter(A("mm"), L("rb", po, FIRST, 16), A("arep", po + 16 * FIRST, po + C))
        if t == 0:
            copy(A("cx2", 0, C, 2), A("cx", 0, H))
            ts(A("cw"), A("cw0"), A("rf", 0, 1), ALU.add)
        if t == 1:
            quant(A("vq"), A("vs"), A("vb"))
        copy(A("ms", 0, 512, 2), A("mm", 1, 512, 2))
        copy(A("ms", 1, 512, 2), A("mm", 0, 512, 2))
        mean(0)
        P, low, twin = ["pa", "pb"], ["lowa", "lowb"], ["lowc", "lowd"]
        side = (po, oo)

        def square(k, h, vector=False):
            o = side[h]
            was = G(A(P[1 - k % 2]), A("ll", 32 * k + o // 16 - 32, 32 * k + o // 16 - 16)) if k else G(A("ms"), L("rb", o))
            if vector:
                copy(A(P[k % 2], o, o + C), was)
            else:
                act(A(P[k % 2], o, o + C), was, ACT.Copy)

        def held(k, h):
            wrap(("xs" if k % 2 else "xs2", side[h]), C, A(P[k % 2], side[h], side[h] + C))

        def listed(k, h):
            unwrap(A("ll", 32 * k + side[h] // 16, 32 * k + side[h] // 16 + 16), ("xs" if k % 2 else "xs2", side[h]), C, C)

        def least(k, h, a=0, b=C):
            a, b = side[h] + a, side[h] + b
            if k:
                tt(A(low[k % 2], a, b), G(A(low[1 - k % 2]), A("ll", 32 * k + a // 16, 32 * k + b // 16)), A(twin[1 - k % 2], a, b), ALU.min)
            else:
                scan(A(low[0], a, b), A("iotaj", a, b), A(P[0], a, b), -1024.0, ALU.max, ALU.min)

        def again(k, h, a=0, b=C, by="scalar"):
            a, b = side[h] + a, side[h] + b
            if by == "vector":
                copy(A(twin[k % 2], a, b), A(low[k % 2], a, b))
            elif by == "pool":
                keep(A(twin[k % 2], a, b), A(low[k % 2], a, b), b - a)
            else:
                act(A(twin[k % 2], a, b), A(low[k % 2], a, b), ACT.Copy)

        square(0, 0, True)
        square(0, 1)
        picked(2)
        wrap(("xs3", 0), C, A("arep", oo, oo + C))
        held(0, 0)
        held(0, 1)
        least(0, 1)
        listed(0, 0)
        listed(0, 1)
        square(1, 1)
        picked(3)
        unpacked(2, True)
        least(0, 0)
        square(1, 0, True)
        again(0, 1, by="pool")
        again(0, 0, by="vector")
        held(1, 0)
        unwrap(L("am", oo), ("xs3", 0), C, C - oo)
        send(t, "am")
        held(1, 1)
        listed(1, 0)
        mean(1)
        listed(1, 1)
        for k in range(1, DOUBLINGS - 1):
            square(k + 1, 0)
            square(k + 1, 1)
            least(k, 0)
            again(k, 0)
            if k == 1:
                least(k, 1, H, C)
                again(k, 1, H, C, "pool")
            held(k + 1, 0)
            least(k, 1, 0, H)
            if k < DOUBLINGS - 2:
                again(k, 1, 0, H)
            listed(k + 1, 0)
            held(k + 1, 1)
            if k > 1:
                least(k, 1, H, C)
            if 1 < k < DOUBLINGS - 2:
                again(k, 1, H, C, "pool")
            if k < 3:
                mean(k + 1)
            listed(k + 1, 1)
        k = DOUBLINGS - 1
        again(k - 1, 1)
        least(k, 0)
        unpacked(3, True)
        again(k, 0)
        least(k, 1)
        again(k, 1)
        quant(A("bq"), A("bs"), A("bt"))
        for b in range(4):
            mm(banks2[b], "eq4", "es", 128 * b, "bq", "bs", 0, C)

        lw, tw = low[1 - DOUBLINGS % 2], twin[1 - DOUBLINGS % 2]

        def fl(o, shift=0):
            return A("fl", 16 + 272 * o // C - shift, 272 + 272 * o // C - shift)

        def flags(o, a=0, b=C):
            f = 16 + 272 * o // C
            tt(A("fl", f + a, f + b), G(A(lw, o, o + C), L("am", o, a // 16, b // 16)), A(tw, o + a, o + b), ALU.is_gt)

        reds = []
        if last:
            reds = [lambda: unwrap(A("wi"), ("xs6", 0), C, 1), lambda: ts(A("nf"), A("wi"), 1, ALU.bitwise_and),
                    lambda: ts(A("hh"), A("wi"), 1, ALU.arith_shift_right), lambda: tt(A("tc"), A("nf"), A("cw"), ALU.mult),
                    lambda: tt(A("lm"), A("tc"), A("hh"), ALU.max), lambda: copy(A("ol16"), A("lm"))]

        def red():
            if reds:
                reds.pop(0)()

        arrive(t, "am")
        flags(po)
        act(A("fa1"), fl(po), ACT.Copy, scale=129.0)
        unpacked(0, False)
        unpacked(1, False)
        flags(oo, 0, H)
        ts(A("fb1", 16, 272), fl(po), -128.0, ALU.mult)
        flags(oo, H, C)
        scan(A("sp"), A("fa1"), A("fb1", 15, 271), 0.0, ALU.add, ALU.add)
        scan(A("vv"), fl(oo), fl(oo, 1), 0.0, ALU.add, ALU.add)
        act(A("ge", H, C), G(A("sp"), A("inl", 8, 16)), ACT.Copy)
        copy(A("ge", 0, H), G(A("sp"), A("inl", 0, 8)))
        unpacked(2, False)
        unpacked(3, False)
        wrap(("xs6", 0), C, A("vv"))
        scan(A("xs5"), A("cx2"), A("ge"), 0.0, ALU.mult, ALU.max)
        unwrap(A("lu", 0, 8), ("xs6", 0), H, 0)
        red()
        ts(A("kl"), A("xs5", 31, C, 32), A("scl2", 0, 1), ALU.mult, -257.0, ALU.add)
        unwrap(A("lu", 8, 16), ("xs6", H), H, 0)
        red()
        red()
        scatter(A("wn"), A("kl"), A("iotaj", 0, H))
        red()
        for h in range(2):
            tt(A("yv", H * h, H * h + H), G(A("wn"), A("lu", 8 * h, 8 * h + 8)), A("iotaj", H + H * h, C + H * h), ALU.min)
        wrap(("xs7", 0), H, A("yv", 0, H))
        red()
        wrap(("xs7", H), H, A("yv", H, C))
        unwrap(A("yl", 0, 8), ("xs7", 0), H, C)
        red()
        unwrap(A("yl", 8, 16), ("xs7", H), H, C)

        def part(h, b, vector):
            win = G(A("dp", 384 * b, 384 * b + 384), A("yl", 8 * h, 8 * h + 8))
            if vector:
                copy(A("yt", 4 * H * h + b, 4 * H * (h + 1), 4), win)
            else:
                act(A("yt", 4 * H * h + b, 4 * H * (h + 1), 4), win, ACT.Copy)

        def packed(h):
            quant(A("zq", H * h, H * h + H), A("zs", H * h, H * h + H), A("yt", 4 * H * h, 4 * H * (h + 1)))

        def products(h):
            for b in (0, 4, 1, 2, 3, 5, 6, 7):
                mm(b, "wq" if b < 4 else "eq4", "wsc" if b < 4 else "es", 128 * (b % 4), "zq", "zs", H * h, H)

        def new(h, b):
            act(A("rr", C * b + H * h, C * b + H * h + H), A("p%d" % b, 0, H), ACT.Relu, scale=0.03125)
            tt(A("xn", 4 * H * h + b, 4 * H * (h + 1), 4), A("p%d" % (4 + b), 0, H), A("rr", C * b + H * h, C * b + H * h + H), ALU.add)

        part(0, 2, False)
        part(0, 3, False)
        part(0, 0, True)
        part(0, 1, True)
        part(1, 0, True)
        packed(0)
        products(0)
        part(1, 3, False)
        part(1, 2, False)
        part(1, 1, True)
        packed(1)
        for b in range(4):
            new(0, b)
        products(1)
        state(t + 1, 0)
        for b in range(4):
            new(1, b)
            if b == 1 and not last:
                scores(t + 1, 0)
        if last:
            result(0)
        else:
            mask(0, 0)
            mask(1, 0)
        state(t + 1, 1)

    result(1)
    for k in range(4):
        dma("sync", T.osc[4 * k:4 * k + 4, :], T["ts%d" % ROUNDS][32 * k:32 * k + 4, 0:C], [A("ts%d" % ROUNDS)], [])
    scatter(A("wo"), A("ol16"), A("iotaj", C, 2 * C))
    dma("sync", T.ol[:, :], T.wo[0:128:16, 1:129], [A("wo")], [])
    emit(g, T, ops, left[0])
